import numpy as np
import ml_dtypes


def mxq(x, axis, fmt="e4m3"):
    dtype, down = {"e4m3": (ml_dtypes.float8_e4m3fn, 7), "e5m2": (ml_dtypes.float8_e5m2, 14)}[fmt]
    v = np.moveaxis(np.asarray(x, np.float32).astype(ml_dtypes.bfloat16).astype(np.float64), axis, -1)
    blocks = v.reshape(v.shape[:-1] + (-1, 32))
    amax = np.abs(blocks).max(-1, keepdims=True)
    byte = np.maximum(np.where(amax > 0, np.frexp(amax)[1] - 1 + 127, 0) - down, 1)
    scale = np.exp2(byte - 127.0)
    codes = (blocks / scale).astype(np.float32).astype(dtype).astype(np.float64)
    return np.moveaxis((codes * scale).reshape(v.shape), -1, axis)


WIDE = False


def mx_kscale(k):
    if not WIDE:
        return np.ones(k)
    levels = np.array([10, -10, 5, -5, 0])
    if k % 512:
        return np.exp2(np.random.permutation(np.resize(levels, k // 32))).repeat(32)
    a = np.empty((k // 512, 16))
    for p in range(k // 512):
        a[p, :8] = np.random.permutation(np.resize(levels, 8))
        for g in range(8):
            far = levels[np.abs(levels - a[p, g]) >= 10]
            a[p, g + 8] = far[np.random.randint(len(far))]
    return np.exp2(a.ravel()).repeat(32)


def f64(x):
    return np.asarray(x).astype(np.float64)


def striped(idx):
    return np.tile(idx.reshape(-1, 16).T, (8, 1)).astype(np.uint16)


def unstriped(offs):
    return offs[:16].T.reshape(-1).astype(np.int64)


E2M1 = np.array([0.0, 0.5, 1.0, 1.5, 2.0, 3.0, 4.0, 6.0, -0.0, -0.5, -1.0, -1.5, -2.0, -3.0, -4.0, -6.0])


def pack_weight(w, fmt):
    k, n = w.shape
    w = f64(np.asarray(w, np.float32).astype(ml_dtypes.bfloat16)).reshape(k // 32, 32, n)
    amax = np.abs(w).max(1)
    if fmt == "e4m3":
        byte = np.frexp(amax)[1] - 1 + 127 - 7
    else:
        mant, ex = np.frexp(amax / 6.0)
        byte = np.where(mant > 0.5, ex, ex - 1) + 127
    byte = np.clip(np.where(amax > 0, byte, 1), 1, 254)
    scaled = (w * np.exp2(127.0 - byte)[:, None, :]).reshape(k, n).astype(np.float32)
    by_word = np.ascontiguousarray(scaled.reshape(k // 512, 128, 4, n).transpose(0, 1, 3, 2))
    if fmt == "e4m3":
        words = by_word.astype(ml_dtypes.float8_e4m3fn).view(np.uint8)
    else:
        c = by_word.astype(ml_dtypes.float4_e2m1fn).view(np.uint8) & 0xF
        words = (c[..., 0::2] | (c[..., 1::2] << 4)).reshape(k // 512, 128, 2 * n)
    return np.ascontiguousarray(words), np.ascontiguousarray(byte.astype(np.uint8).reshape(k // 512, 16, n))


def unpack_weight(words, scales, fmt):
    g, _, n = scales.shape
    words = np.ascontiguousarray(words).reshape(g, 128, n, -1)
    if fmt == "e4m3":
        vals = words.view(ml_dtypes.float8_e4m3fn).astype(np.float64)
    else:
        nib = np.empty((g, 128, n, 4), np.uint8)
        nib[..., 0::2] = words & 0xF
        nib[..., 1::2] = words >> 4
        vals = E2M1[nib]
    vals = vals * np.repeat(np.exp2(scales.astype(np.float64) - 127.0), 8, axis=1)[..., None]
    return vals.transpose(0, 1, 3, 2).reshape(g * 512, n)


def relu2(v):
    return np.maximum(v, 0.0) ** 2


K, T, E, C, H, N = 1536, 768, 6, 128, 512, 256


def by_expert(wq, xq):
    return np.concatenate([wq[e].T @ xq[:, e * C:(e + 1) * C] for e in range(E)], axis=1)


def setup_inputs():
    n = np.random.standard_normal
    s = mx_kscale(K)
    u = mx_kscale(H)
    slot_token = np.random.permutation(T)[:E * C]
    x = pack_weight(n((K, T)) * s[:, None], "e4m3")
    w2 = pack_weight(n((H, N)) / np.sqrt(H) / u[:, None] ** 2, "e4m3")
    return {
        "x_words": x[0],
        "x_scales": x[1],
        "w1": (n((E, K, H)) / np.sqrt(K) / s[None, :, None] * u).astype(np.float32),
        "w2_words": w2[0],
        "w2_scales": w2[1],
        "gate": np.tile(np.random.uniform(0.2, 1.0, E * C), (128, 1)).astype(np.float32),
        "offs": striped(slot_token),
    }


def reference(x_words, x_scales, w1, w2_words, w2_scales, gate, offs):
    w1q = mxq(f64(w1), 1, "e4m3")
    w2 = unpack_weight(w2_words, w2_scales, "e4m3")
    idx = unstriped(offs)
    xq = unpack_weight(x_words, x_scales, "e4m3")[:, idx]
    h = relu2(by_expert(w1q, xq))
    c = np.zeros((H, T))
    c[:, idx] = f64(gate[:1]) * h
    return w2.T @ mxq(c, 0, "e4m3")

@@ -1,0 +1,211 @@
+from contextlib import ExitStack
+
+import concourse.mybir as mybir
+
+K, T, E, C, H, N = 1536, 768, 6, 128, 512, 256
+FLOPS = 2 * K * H * E * C + 2 * H * N * T
+
+F32 = mybir.dt.float32
+BF16 = mybir.dt.bfloat16
+I32 = mybir.dt.int32
+U32 = mybir.dt.uint32
+U16 = mybir.dt.uint16
+U8 = mybir.dt.uint8
+FP8X4 = mybir.dt.float8_e4m3fn_x4
+ACT = mybir.ActivationFunctionType
+ALU = mybir.AluOpType
+
+P = 128
+PASSES = K // 512
+GATHER = 384
+TOK = 256
+VECTOR_CASTS = {(0, 2, 0)} | {(e, s, 0) for e in range(1, E) for s in (0, 2)}
+
+
+def tile_moe_sdn_lin_relu2_kernel(
+    tc, x_words, x_scales, w1, w2_words, w2_scales, gate, offs, out
+):
+    nc = tc.nc
+    with ExitStack() as ctx:
+        keep = ctx.enter_context(tc.tile_pool(name="keep", bufs=1))
+        ring = ctx.enter_context(tc.tile_pool(name="ring", bufs=4))
+        coded = ctx.enter_context(tc.tile_pool(name="coded", bufs=12))
+        psum = ctx.enter_context(tc.psum_pool(name="psum", bufs=1))
+
+        offsets = keep.tile([P, T // 16], U16, name="offsets")
+        nc.sync.dma_start(offsets[:], offs)
+
+        x_plane = keep.tile([P, T // 4], I32, name="x_plane", align_bytes=64)
+        w2_plane = keep.tile([P, N // 4], I32, name="w2_plane", align_bytes=64)
+        nc.vector.memset(x_plane[:], 0)
+        nc.vector.memset(w2_plane[:], 0)
+
+        raw = {}
+
+        def load_w1(e, s, c0, c1):
+            tile = keep.tile([P, 4, c1 - c0], F32, name="raw_%d_%d_%d" % (e, s, c0))
+            rows = w1[e, 512 * s : 512 * (s + 1), :].rearrange("(p j) c -> p j c", j=4)
+            nc.sync.dma_start(tile[:], rows[:, :, c0:c1])
+            raw.setdefault((e, s), []).append((c0, c1, tile))
+
+        x_tile = keep.tile([P, PASSES, T], I32, name="x_tile", align_bytes=64)
+        gate_tile = keep.tile([P, T], F32, name="gate_tile")
+        w2_tile = keep.tile([P, N], I32, name="w2_tile", align_bytes=64)
+        for s in range(PASSES):
+            nc.sync.dma_start(x_tile[:, s, :], x_words[s].rearrange("p t d -> p (t d)").bitcast(I32))
+        for e in range(E):
+            for s in range(PASSES):
+                if (e, s) == (E - 1, PASSES - 1):
+                    load_w1(e, s, 0, H // 2)
+                    load_w1(e, s, H // 2, H)
+                else:
+                    load_w1(e, s, 0, H)
+                if (e, s) == (0, 0):
+                    for q in range(4):
+                        nc.sync.dma_start(
+                            x_plane[32 * q : 32 * q + 4 * PASSES, :], x_scales[:, 4 * q : 4 * q + 4, :].bitcast(I32)
+                        )
+                if (e, s) == (1, 0):
+                    nc.sync.dma_start(gate_tile[:], gate)
+                if (e, s) == (0, 1):
+                    for q in range(4):
+                        nc.sync.dma_start(
+                            w2_plane[32 * q : 32 * q + 4, :], w2_scales[0, 4 * q : 4 * q + 4, :].bitcast(I32)
+                        )
+        nc.sync.dma_start(w2_tile[:], w2_words[0].rearrange("p n d -> p (n d)").bitcast(I32))
+
+        slot_words = keep.tile([P, PASSES, T], U32, name="slot_words", align_bytes=64)
+        slot_plane = keep.tile([P, T], U8, name="slot_plane", align_bytes=64)
+
+        for s in range(PASSES):
+            for a in range(0, T, GATHER):
+                lst = offsets[:, a // 16 : (a + GATHER) // 16]
+                nc.vector.tensor_copy(slot_words[:, s, a : a + GATHER], x_tile[:, s, :].bitcast(U32).indirect(lst))
+        for a in range(0, T, GATHER):
+            lst = offsets[:, a // 16 : (a + GATHER) // 16]
+            nc.vector.tensor_copy(slot_plane[:, a : a + GATHER], x_plane[:].bitcast(U8).indirect(lst))
+
+        codes = {}
+
+        def cast(e, s, u):
+            grouped = ring.tile([P, 2, P, 4], BF16, name="grouped", align_bytes=64)
+            for c0, c1, tile in raw[(e, s)]:
+                src = tile[:].rearrange("p j (m u d) -> p u m j d", u=2, d=2)[:, u]
+                dst = grouped[:, :, c0 // 4 : c1 // 4, :].rearrange("p d m j -> p m j d")
+                if (e, s, u) in VECTOR_CASTS:
+                    nc.vector.tensor_copy(dst, src)
+                else:
+                    nc.scalar.copy(dst, src)
+            return grouped
+
+        def quantize(e, s, u, grouped):
+            words = coded.tile([P, 2 * P], U32, name="w1_words", align_bytes=64)
+            plane = coded.tile([P, 2 * P], U8, name="w1_plane", align_bytes=64)
+            nc.vector.quantize_mx(
+                out=words[:].bitcast(FP8X4), scales=plane[:], in_=grouped[:].rearrange("p d m j -> p (d m j)")
+            )
+            codes[(e, s, u)] = (words, plane)
+
+        def first_product(e, s, t, acc):
+            words, plane = codes[(e, s, t // 2)]
+            cols = slice(P * (t % 2), P * (t % 2 + 1))
+            slots = slice(C * e, C * (e + 1))
+            nc.tensor.matmul_mx(
+                out=acc,
+                lhsT=words[:, cols].bitcast(FP8X4),
+                lhsT_scale=plane[:, cols],
+                rhs=slot_words[:, s, slots].bitcast(FP8X4),
+                rhs_scale=slot_plane[4 * s : P, slots],
+                start=(s == 0),
+                stop=(s == PASSES - 1),
+            )
+
+        windows = [keep.tile([P, T], F32, name="window_%d" % t) for t in range(4)]
+        squares = {}
+
+        def scatter(e, t):
+            lst = offsets[:, C * e // 16 : C * (e + 1) // 16]
+            nc.vector.tensor_tensor(
+                windows[t][:].indirect(lst), squares[(e, t)], gate_tile[:, C * e : C * (e + 1)], ALU.mult
+            )
+
+        last_banks = [psum.tile([P, C], F32, name="last_%d" % t) for t in range(4)]
+        banks = {}
+
+        def multiply(e, s, u):
+            if s == 0:
+                banks[(e, u)] = psum.tile([P, 2, C], F32, name="bank_%d" % (2 * (e % 2) + u))
+            first_product(e, s, 2 * u, banks[(e, u)][:, 0, :])
+            if s == PASSES - 1:
+                for r in range(PASSES):
+                    first_product(e, r, 2 * u + 1, banks[(e, u)][:, 1, :])
+
+        def activate(e):
+            relu = raw[(e + 1, 0)][0][2][:, 0, :].rearrange("p (t n) -> p t n", t=4)
+            squared = ring.tile([P, 4, C], F32, name="squared", bufs=2)
+            for u in range(2):
+                pair = slice(2 * u, 2 * u + 2)
+                nc.scalar.activation(relu[:, pair, :], banks[(e, u)][:], ACT.Relu)
+                nc.scalar.activation(squared[:, pair, :], relu[:, pair, :], ACT.Square)
+            for t in range(4):
+                squares[(e, t)] = squared[:, t, :]
+
+        for e in range(E):
+            for s in range(PASSES):
+                grouped = [cast(e, s, u) for u in range(2)]
+                if e > 0 and s == 0:
+                    activate(e - 1)
+                for u in range(2):
+                    quantize(e, s, u, grouped[u])
+                    if e < E - 1:
+                        multiply(e, s, u)
+                    else:
+                        for t in (2 * u, 2 * u + 1):
+                            first_product(e, s, t, last_banks[t][:])
+                if e > 0 and s == 0:
+                    for t in range(4):
+                        scatter(e - 1, t)
+        relu = ring.tile([P, 4, C], F32, name="relu", bufs=2)
+        squared = ring.tile([P, 4, C], F32, name="squared", bufs=2)
+        for t in range(4):
+            nc.scalar.activation(relu[:, t, :], last_banks[t][:], ACT.Relu)
+            nc.scalar.activation(squared[:, t, :], relu[:, t, :], ACT.Square)
+            squares[(E - 1, t)] = squared[:, t, :]
+            scatter(E - 1, t)
+
+        chunks = T // TOK
+        planes = [keep.tile([P, 4, TOK], BF16, name="planes_%d" % a) for a in range(chunks)]
+        c_in = [keep.tile([P, TOK, 4], BF16, name="c_in_%d" % a, align_bytes=64) for a in range(chunks)]
+        for t in range(4):
+            for a in range(chunks):
+                copy = nc.scalar.copy if t < 3 or a == chunks - 1 else nc.vector.tensor_copy
+                copy(planes[a][:, t, :], windows[t][:, TOK * a : TOK * (a + 1)])
+        for a in range(chunks):
+            copy = nc.scalar.copy if a == chunks - 1 else nc.vector.tensor_copy
+            copy(
+                c_in[a][:].rearrange("p (n i) t -> p n t i", i=4),
+                planes[a][:].rearrange("p t (n i) -> p n t i", i=4),
+            )
+        for a in range(chunks):
+            c_words = keep.tile([P, TOK], U32, name="c_words_%d" % a, align_bytes=64)
+            c_plane = keep.tile([P, TOK], U8, name="c_plane_%d" % a, align_bytes=64)
+            nc.vector.quantize_mx(
+                out=c_words[:].bitcast(FP8X4),
+                scales=c_plane[:],
+                in_=c_in[a][:].rearrange("p n t -> p (n t)"),
+            )
+            acc = psum.tile([P, 2, TOK], F32, name="bank_%d" % a)
+            for h in range(2):
+                nc.tensor.matmul_mx(
+                    out=acc[:, h, :],
+                    lhsT=w2_tile[:, P * h : P * (h + 1)].bitcast(FP8X4),
+                    lhsT_scale=w2_plane[:].bitcast(U8)[:, P * h : P * (h + 1)],
+                    rhs=c_words[:].bitcast(FP8X4),
+                    rhs_scale=c_plane[:],
+                    start=True,
+                    stop=True,
+                )
+            result = keep.tile([P, 2, TOK], F32, name="result_%d" % a)
+            copy = nc.vector.tensor_copy if a == chunks - 1 else nc.scalar.copy
+            copy(result[:], acc[:])
+            nc.sync.dma_start(out.rearrange("(h p) t -> p h t", h=2)[:, :, TOK * a : TOK * (a + 1)], result[:])

@@ -18,8 +18,10 @@ ALU = mybir.AluOpType
 P = 128
 PASSES = K // 512
 GATHER = 384
-TOK = 256
-VECTOR_CASTS = {(0, 2, 0)} | {(e, s, 0) for e in range(1, E) for s in (0, 2)}
+VECTOR_CASTS = {(0, 1, 0, 0), (0, 2, 0, 0), (5, 2, 1, 0)} | {(e, s, 0, 0) for e in range(1, E) for s in (0, 1)}
+WIDE = {(e, s) for e in range(1, E) for s in (0, 1)} - {(E - 1, 0)}
+SPLIT = 512
+CHUNKS = [(0, 128), (512, 640), (128, 384), (384, 512), (640, 768)]
 
 
 def tile_moe_sdn_lin_relu2_kernel(
@@ -29,7 +31,7 @@ def tile_moe_sdn_lin_relu2_kernel(
     with ExitStack() as ctx:
         keep = ctx.enter_context(tc.tile_pool(name="keep", bufs=1))
         ring = ctx.enter_context(tc.tile_pool(name="ring", bufs=4))
-        coded = ctx.enter_context(tc.tile_pool(name="coded", bufs=12))
+        coded = ctx.enter_context(tc.tile_pool(name="coded", bufs=5))
         psum = ctx.enter_context(tc.psum_pool(name="psum", bufs=1))
 
         offsets = keep.tile([P, T // 16], U16, name="offsets")
@@ -49,7 +51,7 @@ def tile_moe_sdn_lin_relu2_kernel(
             raw.setdefault((e, s), []).append((c0, c1, tile))
 
         x_tile = keep.tile([P, PASSES, T], I32, name="x_tile", align_bytes=64)
-        gate_tile = keep.tile([P, T], F32, name="gate_tile")
+        gates = [keep.tile([P, C], F32, name="gate_%d" % e) for e in range(E)]
         w2_tile = keep.tile([P, N], I32, name="w2_tile", align_bytes=64)
         for s in range(PASSES):
             nc.sync.dma_start(x_tile[:, s, :], x_words[s].rearrange("p t d -> p (t d)").bitcast(I32))
@@ -65,14 +67,12 @@ def tile_moe_sdn_lin_relu2_kernel(
                         nc.sync.dma_start(
                             x_plane[32 * q : 32 * q + 4 * PASSES, :], x_scales[:, 4 * q : 4 * q + 4, :].bitcast(I32)
                         )
-                if (e, s) == (1, 0):
-                    nc.sync.dma_start(gate_tile[:], gate)
-                if (e, s) == (0, 1):
-                    for q in range(4):
-                        nc.sync.dma_start(
-                            w2_plane[32 * q : 32 * q + 4, :], w2_scales[0, 4 * q : 4 * q + 4, :].bitcast(I32)
-                        )
+                if e > 0 and s == 1:
+                    nc.sync.dma_start(gates[e - 1][:], gate[:, C * (e - 1) : C * e])
+        nc.sync.dma_start(gates[E - 1][:], gate[:, C * (E - 1) : C * E])
         nc.sync.dma_start(w2_tile[:], w2_words[0].rearrange("p n d -> p (n d)").bitcast(I32))
+        for q in range(4):
+            nc.sync.dma_start(w2_plane[32 * q : 32 * q + 4, :], w2_scales[0, 4 * q : 4 * q + 4, :].bitcast(I32))
 
         slot_words = keep.tile([P, PASSES, T], U32, name="slot_words", align_bytes=64)
         slot_plane = keep.tile([P, T], U8, name="slot_plane", align_bytes=64)
@@ -87,28 +87,33 @@ def tile_moe_sdn_lin_relu2_kernel(
 
         codes = {}
 
-        def cast(e, s, u):
-            grouped = ring.tile([P, 2, P, 4], BF16, name="grouped", align_bytes=64)
+        def cast(e, s):
+            grouped = ring.tile([P, 4, P, 4], BF16, name="grouped", align_bytes=64)
             for c0, c1, tile in raw[(e, s)]:
-                src = tile[:].rearrange("p j (m u d) -> p u m j d", u=2, d=2)[:, u]
-                dst = grouped[:, :, c0 // 4 : c1 // 4, :].rearrange("p d m j -> p m j d")
-                if (e, s, u) in VECTOR_CASTS:
-                    nc.vector.tensor_copy(dst, src)
-                else:
-                    nc.scalar.copy(dst, src)
+                for u in range(2):
+                    src = tile[:].rearrange("p j (m u d) -> p u m j d", u=2, d=2)[:, u]
+                    dst = grouped[:, 2 * u : 2 * u + 2, c0 // 4 : c1 // 4, :].rearrange("p d m j -> p m j d")
+                    if (e, s, u, c0) in VECTOR_CASTS:
+                        nc.vector.tensor_copy(dst, src)
+                    else:
+                        nc.scalar.copy(dst, src)
             return grouped
 
-        def quantize(e, s, u, grouped):
-            words = coded.tile([P, 2 * P], U32, name="w1_words", align_bytes=64)
-            plane = coded.tile([P, 2 * P], U8, name="w1_plane", align_bytes=64)
+        def quantize(e, s, t0, t1, grouped):
+            if t0 == 0:
+                words = coded.tile([P, H], U32, name="w1_words", align_bytes=64)
+                plane = coded.tile([P, H], U8, name="w1_plane", align_bytes=64)
+                codes[(e, s)] = (words, plane)
+            words, plane = codes[(e, s)]
             nc.vector.quantize_mx(
-                out=words[:].bitcast(FP8X4), scales=plane[:], in_=grouped[:].rearrange("p d m j -> p (d m j)")
+                out=words[:, P * t0 : P * t1].bitcast(FP8X4),
+                scales=plane[:, P * t0 : P * t1],
+                in_=grouped[:, t0:t1].rearrange("p t m j -> p (t m j)"),
             )
-            codes[(e, s, u)] = (words, plane)
 
         def first_product(e, s, t, acc):
-            words, plane = codes[(e, s, t // 2)]
-            cols = slice(P * (t % 2), P * (t % 2 + 1))
+            words, plane = codes[(e, s)]
+            cols = slice(P * t, P * (t + 1))
             slots = slice(C * e, C * (e + 1))
             nc.tensor.matmul_mx(
                 out=acc,
@@ -126,7 +131,7 @@ def tile_moe_sdn_lin_relu2_kernel(
         def scatter(e, t):
             lst = offsets[:, C * e // 16 : C * (e + 1) // 16]
             nc.vector.tensor_tensor(
-                windows[t][:].indirect(lst), squares[(e, t)], gate_tile[:, C * e : C * (e + 1)], ALU.mult
+                windows[t][:].indirect(lst), squares[(e, t)], gates[e][:], ALU.mult
             )
 
         last_banks = [psum.tile([P, C], F32, name="last_%d" % t) for t in range(4)]
@@ -143,29 +148,38 @@ def tile_moe_sdn_lin_relu2_kernel(
         def activate(e):
             relu = raw[(e + 1, 0)][0][2][:, 0, :].rearrange("p (t n) -> p t n", t=4)
             squared = ring.tile([P, 4, C], F32, name="squared", bufs=2)
+            for t in range(4):
+                squares[(e, t)] = squared[:, t, :]
             for u in range(2):
                 pair = slice(2 * u, 2 * u + 2)
                 nc.scalar.activation(relu[:, pair, :], banks[(e, u)][:], ACT.Relu)
+                if (e, u) == (E - 2, 1):
+                    pair = slice(2, 3)
                 nc.scalar.activation(squared[:, pair, :], relu[:, pair, :], ACT.Square)
-            for t in range(4):
-                squares[(e, t)] = squared[:, t, :]
+            return relu
 
         for e in range(E):
             for s in range(PASSES):
-                grouped = [cast(e, s, u) for u in range(2)]
+                grouped = cast(e, s)
                 if e > 0 and s == 0:
-                    activate(e - 1)
+                    relu = activate(e - 1)
+                if e > 0 and s == 1:
+                    for t in range(4 if e < E - 1 else 3):
+                        scatter(e - 1, t)
+                if (e, s) in WIDE:
+                    quantize(e, s, 0, 4, grouped)
                 for u in range(2):
-                    quantize(e, s, u, grouped[u])
+                    if (e, s) not in WIDE:
+                        quantize(e, s, 2 * u, 2 * u + 2, grouped)
                     if e < E - 1:
                         multiply(e, s, u)
                     else:
                         for t in (2 * u, 2 * u + 1):
                             first_product(e, s, t, last_banks[t][:])
-                if e > 0 and s == 0:
-                    for t in range(4):
-                        scatter(e - 1, t)
-        relu = ring.tile([P, 4, C], F32, name="relu", bufs=2)
+        squares[(E - 2, 3)] = raw[(E - 1, PASSES - 1)][1][2][:, 0, 0:C]
+        nc.scalar.activation(squares[(E - 2, 3)], relu[:, 3, :], ACT.Square)
+        scatter(E - 2, 3)
+        relu = ring.tile([P, 4, C], F32, name="relu", bufs=1)
         squared = ring.tile([P, 4, C], F32, name="squared", bufs=2)
         for t in range(4):
             nc.scalar.activation(relu[:, t, :], last_banks[t][:], ACT.Relu)
@@ -173,31 +187,29 @@ def tile_moe_sdn_lin_relu2_kernel(
             squares[(E - 1, t)] = squared[:, t, :]
             scatter(E - 1, t)
 
-        chunks = T // TOK
-        planes = [keep.tile([P, 4, TOK], BF16, name="planes_%d" % a) for a in range(chunks)]
-        c_in = [keep.tile([P, TOK, 4], BF16, name="c_in_%d" % a, align_bytes=64) for a in range(chunks)]
+        shares = [(0, SPLIT, nc.vector.tensor_copy), (SPLIT, T, nc.scalar.copy)]
+        planes = [keep.tile([P, 4, b - a], BF16, name="planes_%d" % a) for a, b, copy in shares]
         for t in range(4):
-            for a in range(chunks):
-                copy = nc.scalar.copy if t < 3 or a == chunks - 1 else nc.vector.tensor_copy
-                copy(planes[a][:, t, :], windows[t][:, TOK * a : TOK * (a + 1)])
-        for a in range(chunks):
-            copy = nc.scalar.copy if a == chunks - 1 else nc.vector.tensor_copy
+            for (a, b, copy), tile in zip(shares, planes):
+                (nc.scalar.copy if t < 3 else copy)(tile[:, t, :], windows[t][:, a:b])
+        bank_names = ["bank_%d" % i for i in range(4)] + ["last_%d" % i for i in range(4)]
+        for i, (a, b) in enumerate(CHUNKS):
+            first, end, copy = shares[a // SPLIT]
+            c_in = keep.tile([P, b - a, 4], BF16, name="c_in_%d" % a, align_bytes=64)
             copy(
-                c_in[a][:].rearrange("p (n i) t -> p n t i", i=4),
-                planes[a][:].rearrange("p t (n i) -> p n t i", i=4),
+                c_in[:].rearrange("p (n i) t -> p n t i", i=4),
+                planes[a // SPLIT][:, :, a - first : b - first].rearrange("p t (n i) -> p n t i", i=4),
             )
-        for a in range(chunks):
-            c_words = keep.tile([P, TOK], U32, name="c_words_%d" % a, align_bytes=64)
-            c_plane = keep.tile([P, TOK], U8, name="c_plane_%d" % a, align_bytes=64)
+            c_words = keep.tile([P, b - a], U32, name="c_words_%d" % a, align_bytes=64)
+            c_plane = keep.tile([P, b - a], U8, name="c_plane_%d" % a, align_bytes=64)
             nc.vector.quantize_mx(
-                out=c_words[:].bitcast(FP8X4),
-                scales=c_plane[:],
-                in_=c_in[a][:].rearrange("p n t -> p (n t)"),
+                out=c_words[:].bitcast(FP8X4), scales=c_plane[:], in_=c_in[:].rearrange("p n t -> p (n t)")
             )
-            acc = psum.tile([P, 2, TOK], F32, name="bank_%d" % a)
-            for h in range(2):
+            result = keep.tile([P, 2, b - a], F32, name="result_%d" % a)
+            for h, empty in enumerate((nc.scalar.copy, nc.vector.tensor_copy)):
+                acc = psum.tile([P, b - a], F32, name=bank_names[(2 * i + h) % 8])
                 nc.tensor.matmul_mx(
-                    out=acc[:, h, :],
+                    out=acc[:],
                     lhsT=w2_tile[:, P * h : P * (h + 1)].bitcast(FP8X4),
                     lhsT_scale=w2_plane[:].bitcast(U8)[:, P * h : P * (h + 1)],
                     rhs=c_words[:].bitcast(FP8X4),
@@ -205,7 +217,5 @@ def tile_moe_sdn_lin_relu2_kernel(
                     start=True,
                     stop=True,
                 )
-            result = keep.tile([P, 2, TOK], F32, name="result_%d" % a)
-            copy = nc.vector.tensor_copy if a == chunks - 1 else nc.scalar.copy
-            copy(result[:], acc[:])
-            nc.sync.dma_start(out.rearrange("(h p) t -> p h t", h=2)[:, :, TOK * a : TOK * (a + 1)], result[:])
+                empty(result[:, h, :], acc[:])
+            nc.sync.dma_start(out.rearrange("(h p) t -> p h t", h=2)[:, :, a:b], result[:])

@@ -18,10 +18,10 @@ ALU = mybir.AluOpType
 P = 128
 PASSES = K // 512
 GATHER = 384
-VECTOR_CASTS = {(0, 1, 0, 0), (0, 2, 0, 0), (5, 2, 1, 0)} | {(e, s, 0, 0) for e in range(1, E) for s in (0, 1)}
+VECTOR_CASTS = {(0, 1, 0, 0), (0, 2, 0, 0), (5, 2, 1, 256)} | {(e, s, 0, 0) for e in range(1, E) for s in (0, 1)}
 WIDE = {(e, s) for e in range(1, E) for s in (0, 1)} - {(E - 1, 0)}
 SPLIT = 512
-CHUNKS = [(0, 128), (512, 640), (128, 384), (384, 512), (640, 768)]
+CHUNKS = [(0, False), (128, False), (256, True), (512, False), (384, True), (640, True)]
 
 
 def tile_moe_sdn_lin_relu2_kernel(
@@ -44,11 +44,9 @@ def tile_moe_sdn_lin_relu2_kernel(
 
         raw = {}
 
-        def load_w1(e, s, c0, c1):
-            tile = keep.tile([P, 4, c1 - c0], F32, name="raw_%d_%d_%d" % (e, s, c0))
-            rows = w1[e, 512 * s : 512 * (s + 1), :].rearrange("(p j) c -> p j c", j=4)
-            nc.sync.dma_start(tile[:], rows[:, :, c0:c1])
-            raw.setdefault((e, s), []).append((c0, c1, tile))
+        def load_w1(e, s):
+            raw[(e, s)] = keep.tile([P, 4, H], F32, name="raw_%d_%d" % (e, s))
+            nc.sync.dma_start(raw[(e, s)][:], w1[e, 512 * s : 512 * (s + 1), :].rearrange("(p j) c -> p j c", j=4))
 
         x_tile = keep.tile([P, PASSES, T], I32, name="x_tile", align_bytes=64)
         gates = [keep.tile([P, C], F32, name="gate_%d" % e) for e in range(E)]
@@ -57,11 +55,7 @@ def tile_moe_sdn_lin_relu2_kernel(
             nc.sync.dma_start(x_tile[:, s, :], x_words[s].rearrange("p t d -> p (t d)").bitcast(I32))
         for e in range(E):
             for s in range(PASSES):
-                if (e, s) == (E - 1, PASSES - 1):
-                    load_w1(e, s, 0, H // 2)
-                    load_w1(e, s, H // 2, H)
-                else:
-                    load_w1(e, s, 0, H)
+                load_w1(e, s)
                 if (e, s) == (0, 0):
                     for q in range(4):
                         nc.sync.dma_start(
@@ -89,9 +83,9 @@ def tile_moe_sdn_lin_relu2_kernel(
 
         def cast(e, s):
             grouped = ring.tile([P, 4, P, 4], BF16, name="grouped", align_bytes=64)
-            for c0, c1, tile in raw[(e, s)]:
-                for u in range(2):
-                    src = tile[:].rearrange("p j (m u d) -> p u m j d", u=2, d=2)[:, u]
+            for u in range(2):
+                for c0, c1 in [(0, H // 2), (H // 2, H)] if (e, s, u) == (E - 1, PASSES - 1, 1) else [(0, H)]:
+                    src = raw[(e, s)][:, :, c0:c1].rearrange("p j (m u d) -> p u m j d", u=2, d=2)[:, u]
                     dst = grouped[:, 2 * u : 2 * u + 2, c0 // 4 : c1 // 4, :].rearrange("p d m j -> p m j d")
                     if (e, s, u, c0) in VECTOR_CASTS:
                         nc.vector.tensor_copy(dst, src)
@@ -146,7 +140,7 @@ def tile_moe_sdn_lin_relu2_kernel(
                     first_product(e, r, 2 * u + 1, banks[(e, u)][:, 1, :])
 
         def activate(e):
-            relu = raw[(e + 1, 0)][0][2][:, 0, :].rearrange("p (t n) -> p t n", t=4)
+            relu = raw[(e + 1, 0)][:, 0, :].rearrange("p (t n) -> p t n", t=4)
             squared = ring.tile([P, 4, C], F32, name="squared", bufs=2)
             for t in range(4):
                 squares[(e, t)] = squared[:, t, :]
@@ -176,7 +170,7 @@ def tile_moe_sdn_lin_relu2_kernel(
                     else:
                         for t in (2 * u, 2 * u + 1):
                             first_product(e, s, t, last_banks[t][:])
-        squares[(E - 2, 3)] = raw[(E - 1, PASSES - 1)][1][2][:, 0, 0:C]
+        squares[(E - 2, 3)] = raw[(E - 1, PASSES - 1)][:, 0, 0:C]
         nc.scalar.activation(squares[(E - 2, 3)], relu[:, 3, :], ACT.Square)
         scatter(E - 2, 3)
         relu = ring.tile([P, 4, C], F32, name="relu", bufs=1)
@@ -193,7 +187,9 @@ def tile_moe_sdn_lin_relu2_kernel(
             for (a, b, copy), tile in zip(shares, planes):
                 (nc.scalar.copy if t < 3 else copy)(tile[:, t, :], windows[t][:, a:b])
         bank_names = ["bank_%d" % i for i in range(4)] + ["last_%d" % i for i in range(4)]
-        for i, (a, b) in enumerate(CHUNKS):
+        used = 0
+        for a, halved in CHUNKS:
+            b = a + C
             first, end, copy = shares[a // SPLIT]
             c_in = keep.tile([P, b - a, 4], BF16, name="c_in_%d" % a, align_bytes=64)
             copy(
@@ -206,10 +202,16 @@ def tile_moe_sdn_lin_relu2_kernel(
                 out=c_words[:].bitcast(FP8X4), scales=c_plane[:], in_=c_in[:].rearrange("p n t -> p (n t)")
             )
             result = keep.tile([P, 2, b - a], F32, name="result_%d" % a)
-            for h, empty in enumerate((nc.scalar.copy, nc.vector.tensor_copy)):
-                acc = psum.tile([P, b - a], F32, name=bank_names[(2 * i + h) % 8])
+            if halved:
+                accs = [psum.tile([P, C], F32, name=bank_names[(used + h) % 8])[:] for h in range(2)]
+                used += 2
+            else:
+                bank = psum.tile([P, 2, C], F32, name=bank_names[used % 8])
+                accs = [bank[:, h, :] for h in range(2)]
+                used += 1
+            for h in range(2):
                 nc.tensor.matmul_mx(
-                    out=acc[:],
+                    out=accs[h],
                     lhsT=w2_tile[:, P * h : P * (h + 1)].bitcast(FP8X4),
                     lhsT_scale=w2_plane[:].bitcast(U8)[:, P * h : P * (h + 1)],
                     rhs=c_words[:].bitcast(FP8X4),
@@ -217,5 +219,9 @@ def tile_moe_sdn_lin_relu2_kernel(
                     start=True,
                     stop=True,
                 )
-                empty(result[:, h, :], acc[:])
+            if halved:
+                nc.scalar.copy(result[:, 0, :], accs[0])
+                nc.vector.tensor_copy(result[:, 1, :], accs[1])
+            else:
+                nc.scalar.copy(result[:], bank[:])
             nc.sync.dma_start(out.rearrange("(h p) t -> p h t", h=2)[:, :, a:b], result[:])

@@ -1,6 +1,7 @@
 from contextlib import ExitStack
 
 import concourse.mybir as mybir
+from concourse.masks import make_identity
 
 K, T, E, C, H, N = 1536, 768, 6, 128, 512, 256
 FLOPS = 2 * K * H * E * C + 2 * H * N * T
@@ -18,10 +19,8 @@ ALU = mybir.AluOpType
 P = 128
 PASSES = K // 512
 GATHER = 384
-VECTOR_CASTS = {(0, 1, 0, 0), (0, 2, 0, 0), (5, 2, 1, 256)} | {(e, s, 0, 0) for e in range(1, E) for s in (0, 1)}
-WIDE = {(e, s) for e in range(1, E) for s in (0, 1)} - {(E - 1, 0)}
-SPLIT = 512
-CHUNKS = [(0, False), (128, False), (256, True), (512, False), (384, True), (640, True)]
+VECTOR_SHARE = 48
+TOKEN_CHUNKS = [256, 256, 128, 128]
 
 
 def tile_moe_sdn_lin_relu2_kernel(
@@ -31,46 +30,42 @@ def tile_moe_sdn_lin_relu2_kernel(
     with ExitStack() as ctx:
         keep = ctx.enter_context(tc.tile_pool(name="keep", bufs=1))
         ring = ctx.enter_context(tc.tile_pool(name="ring", bufs=4))
-        coded = ctx.enter_context(tc.tile_pool(name="coded", bufs=5))
-        psum = ctx.enter_context(tc.psum_pool(name="psum", bufs=1))
+        psum = ctx.enter_context(tc.psum_pool(name="psum", bufs=2))
 
         offsets = keep.tile([P, T // 16], U16, name="offsets")
         nc.sync.dma_start(offsets[:], offs)
 
         x_plane = keep.tile([P, T // 4], I32, name="x_plane", align_bytes=64)
         w2_plane = keep.tile([P, N // 4], I32, name="w2_plane", align_bytes=64)
+        gate_rows = keep.tile([P, C], F32, name="gate_rows")
+        identity = keep.tile([P, P], F32, name="identity")
         nc.vector.memset(x_plane[:], 0)
         nc.vector.memset(w2_plane[:], 0)
-
-        raw = {}
-
-        def load_w1(e, s):
-            raw[(e, s)] = keep.tile([P, 4, H], F32, name="raw_%d_%d" % (e, s))
-            nc.sync.dma_start(raw[(e, s)][:], w1[e, 512 * s : 512 * (s + 1), :].rearrange("(p j) c -> p j c", j=4))
+        nc.vector.memset(gate_rows[:], 0.0)
+        make_identity(nc, identity[:])
 
         x_tile = keep.tile([P, PASSES, T], I32, name="x_tile", align_bytes=64)
-        gates = [keep.tile([P, C], F32, name="gate_%d" % e) for e in range(E)]
         w2_tile = keep.tile([P, N], I32, name="w2_tile", align_bytes=64)
         for s in range(PASSES):
             nc.sync.dma_start(x_tile[:, s, :], x_words[s].rearrange("p t d -> p (t d)").bitcast(I32))
+        raw = {}
         for e in range(E):
             for s in range(PASSES):
-                load_w1(e, s)
+                raw[(e, s)] = keep.tile([P, 4, H], F32, name="raw_%d_%d" % (e, s))
+                nc.sync.dma_start(raw[(e, s)][:], w1[e, 512 * s : 512 * (s + 1), :].rearrange("(p j) c -> p j c", j=4))
                 if (e, s) == (0, 0):
                     for q in range(4):
                         nc.sync.dma_start(
                             x_plane[32 * q : 32 * q + 4 * PASSES, :], x_scales[:, 4 * q : 4 * q + 4, :].bitcast(I32)
                         )
-                if e > 0 and s == 1:
-                    nc.sync.dma_start(gates[e - 1][:], gate[:, C * (e - 1) : C * e])
-        nc.sync.dma_start(gates[E - 1][:], gate[:, C * (E - 1) : C * E])
+                if (e, s) == (0, 2):
+                    nc.sync.dma_start(gate_rows[0:E, :], gate[0].rearrange("(e c) -> e c", e=E))
         nc.sync.dma_start(w2_tile[:], w2_words[0].rearrange("p n d -> p (n d)").bitcast(I32))
         for q in range(4):
             nc.sync.dma_start(w2_plane[32 * q : 32 * q + 4, :], w2_scales[0, 4 * q : 4 * q + 4, :].bitcast(I32))
 
         slot_words = keep.tile([P, PASSES, T], U32, name="slot_words", align_bytes=64)
         slot_plane = keep.tile([P, T], U8, name="slot_plane", align_bytes=64)
-
         for s in range(PASSES):
             for a in range(0, T, GATHER):
                 lst = offsets[:, a // 16 : (a + GATHER) // 16]
@@ -79,139 +74,114 @@ def tile_moe_sdn_lin_relu2_kernel(
             lst = offsets[:, a // 16 : (a + GATHER) // 16]
             nc.vector.tensor_copy(slot_plane[:, a : a + GATHER], x_plane[:].bitcast(U8).indirect(lst))
 
-        codes = {}
+        gate_bank = psum.tile([P, 2, C], F32, name="turned")
+        nc.tensor.transpose(gate_bank[:, 0, :], gate_rows[:], identity[:])
+        gate_columns = keep.tile([P, 8], F32, name="gate_columns")
+        nc.scalar.copy(gate_columns[:], gate_bank[:, 0, 0:8])
 
-        def cast(e, s):
-            grouped = ring.tile([P, 4, P, 4], BF16, name="grouped", align_bytes=64)
-            for u in range(2):
-                for c0, c1 in [(0, H // 2), (H // 2, H)] if (e, s, u) == (E - 1, PASSES - 1, 1) else [(0, H)]:
-                    src = raw[(e, s)][:, :, c0:c1].rearrange("p j (m u d) -> p u m j d", u=2, d=2)[:, u]
-                    dst = grouped[:, 2 * u : 2 * u + 2, c0 // 4 : c1 // 4, :].rearrange("p d m j -> p m j d")
-                    if (e, s, u, c0) in VECTOR_CASTS:
-                        nc.vector.tensor_copy(dst, src)
-                    else:
-                        nc.scalar.copy(dst, src)
-            return grouped
-
-        def quantize(e, s, t0, t1, grouped):
-            if t0 == 0:
-                words = coded.tile([P, H], U32, name="w1_words", align_bytes=64)
-                plane = coded.tile([P, H], U8, name="w1_plane", align_bytes=64)
-                codes[(e, s)] = (words, plane)
-            words, plane = codes[(e, s)]
-            nc.vector.quantize_mx(
-                out=words[:, P * t0 : P * t1].bitcast(FP8X4),
-                scales=plane[:, P * t0 : P * t1],
-                in_=grouped[:, t0:t1].rearrange("p t m j -> p (t m j)"),
+        def cast(e, s, grouped, u0, u1, m0, m1, copy):
+            copy(
+                grouped[:, u0:u1, m0:m1].rearrange("p u m d j -> p m j u d"),
+                raw[(e, s)][:].rearrange("p j (m u d) -> p m j u d", u=2, d=2)[:, m0:m1, :, u0:u1],
             )
 
-        def first_product(e, s, t, acc):
-            words, plane = codes[(e, s)]
-            cols = slice(P * t, P * (t + 1))
+        def quantize(grouped, words, plane, u0, u1):
+            cols = slice(2 * P * u0, 2 * P * u1)
+            nc.vector.quantize_mx(
+                out=words[:, cols].bitcast(FP8X4),
+                scales=plane[:, cols],
+                in_=grouped[:, u0:u1].rearrange("p u m d j -> p (u m d j)"),
+            )
+
+        def multiply(e, s, words, plane, u0, u1, acc):
             slots = slice(C * e, C * (e + 1))
+            cols = slice(2 * P * u0, 2 * P * u1)
             nc.tensor.matmul_mx(
                 out=acc,
-                lhsT=words[:, cols].bitcast(FP8X4),
-                lhsT_scale=plane[:, cols],
-                rhs=slot_words[:, s, slots].bitcast(FP8X4),
-                rhs_scale=slot_plane[4 * s : P, slots],
+                lhsT=slot_words[:, s, slots].bitcast(FP8X4),
+                lhsT_scale=slot_plane[4 * s : P, slots],
+                rhs=words[:, cols].bitcast(FP8X4),
+                rhs_scale=plane[:, cols],
                 start=(s == 0),
                 stop=(s == PASSES - 1),
             )
 
-        windows = [keep.tile([P, T], F32, name="window_%d" % t) for t in range(4)]
-        squares = {}
+        windows = [keep.tile([P, T], F32, name="window_%d" % u) for u in range(2)]
 
-        def scatter(e, t):
-            lst = offsets[:, C * e // 16 : C * (e + 1) // 16]
-            nc.vector.tensor_tensor(
-                windows[t][:].indirect(lst), squares[(e, t)], gates[e][:], ALU.mult
-            )
+        def activate(e, acc, halves, relu, turned):
+            nc.scalar.activation(relu, acc, ACT.Relu)
+            gated = ring.tile([P, 2 * P * halves], BF16, name="gated", bufs=2)
+            nc.vector.scalar_tensor_tensor(gated[:], relu, gate_columns[:, e : e + 1], relu, ALU.mult, ALU.mult)
+            for u in range(halves):
+                cols = slice(P * u, P * (u + 1))
+                nc.tensor.transpose(turned[:, cols], gated[:].bitcast(F32)[:, cols], identity[:])
 
-        last_banks = [psum.tile([P, C], F32, name="last_%d" % t) for t in range(4)]
-        banks = {}
+        def scatter(e, u, turned, pairs):
+            nc.scalar.copy(pairs, turned)
+            nc.vector.tensor_copy(windows[u][:].indirect(offsets[:, C * e // 16 : C * (e + 1) // 16]), pairs)
 
-        def multiply(e, s, u):
-            if s == 0:
-                banks[(e, u)] = psum.tile([P, 2, C], F32, name="bank_%d" % (2 * (e % 2) + u))
-            first_product(e, s, 2 * u, banks[(e, u)][:, 0, :])
-            if s == PASSES - 1:
-                for r in range(PASSES):
-                    first_product(e, r, 2 * u + 1, banks[(e, u)][:, 1, :])
-
-        def activate(e):
-            relu = raw[(e + 1, 0)][:, 0, :].rearrange("p (t n) -> p t n", t=4)
-            squared = ring.tile([P, 4, C], F32, name="squared", bufs=2)
-            for t in range(4):
-                squares[(e, t)] = squared[:, t, :]
-            for u in range(2):
-                pair = slice(2 * u, 2 * u + 2)
-                nc.scalar.activation(relu[:, pair, :], banks[(e, u)][:], ACT.Relu)
-                if (e, u) == (E - 2, 1):
-                    pair = slice(2, 3)
-                nc.scalar.activation(squared[:, pair, :], relu[:, pair, :], ACT.Square)
-            return relu
-
+        last_accs = [psum.tile([P, H // 2], F32, name="last_acc_%d" % u, bufs=1) for u in range(2)]
         for e in range(E):
+            previous = acc if e > 0 else None
+            if e < E - 1:
+                acc = psum.tile([P, H], F32, name="acc")
             for s in range(PASSES):
-                grouped = cast(e, s)
+                grouped = ring.tile([P, 2, P, 2, 4], BF16, name="grouped", align_bytes=64)
+                words = ring.tile([P, H], U32, name="w1_words", align_bytes=64)
+                plane = ring.tile([P, H], U8, name="w1_plane", align_bytes=64)
+                split = 64 if (e, s) == (E - 1, 1) else VECTOR_SHARE
+                if (e, s) == (E - 1, PASSES - 1):
+                    cast(e, s, grouped, 0, 1, 0, P, nc.vector.tensor_copy)
+                    cast(e, s, grouped, 1, 2, 0, 32, nc.vector.tensor_copy)
+                    cast(e, s, grouped, 1, 2, 32, P, nc.scalar.copy)
+                    for u in range(2):
+                        quantize(grouped, words, plane, u, u + 1)
+                else:
+                    if e == 0 and s < 2:
+                        split = 0
+                    if split > 0:
+                        cast(e, s, grouped, 0, 2, 0, split, nc.vector.tensor_copy)
+                    cast(e, s, grouped, 0, 2, split, P, nc.scalar.copy)
+                    quantize(grouped, words, plane, 0, 2)
+                if e < E - 1:
+                    multiply(e, s, words, plane, 0, 2, acc[:])
+                else:
+                    for u in range(2):
+                        multiply(e, s, words, plane, u, u + 1, last_accs[u][:])
                 if e > 0 and s == 0:
-                    relu = activate(e - 1)
-                if e > 0 and s == 1:
-                    for t in range(4 if e < E - 1 else 3):
-                        scatter(e - 1, t)
-                if (e, s) in WIDE:
-                    quantize(e, s, 0, 4, grouped)
-                for u in range(2):
-                    if (e, s) not in WIDE:
-                        quantize(e, s, 2 * u, 2 * u + 2, grouped)
-                    if e < E - 1:
-                        multiply(e, s, u)
-                    else:
-                        for t in (2 * u, 2 * u + 1):
-                            first_product(e, s, t, last_banks[t][:])
-        squares[(E - 2, 3)] = raw[(E - 1, PASSES - 1)][:, 0, 0:C]
-        nc.scalar.activation(squares[(E - 2, 3)], relu[:, 3, :], ACT.Square)
-        scatter(E - 2, 3)
-        relu = ring.tile([P, 4, C], F32, name="relu", bufs=1)
-        squared = ring.tile([P, 4, C], F32, name="squared", bufs=2)
-        for t in range(4):
-            nc.scalar.activation(relu[:, t, :], last_banks[t][:], ACT.Relu)
-            nc.scalar.activation(squared[:, t, :], relu[:, t, :], ACT.Square)
-            squares[(E - 1, t)] = squared[:, t, :]
-            scatter(E - 1, t)
+                    turned = psum.tile([P, 2 * C], F32, name="turned")
+                    activate(e - 1, previous[:], 2, raw[(e, s)][:, 0, :], turned)
+                if 0 < e < E - 1 and s > 0:
+                    scatter(e - 1, s - 1, turned[:, C * (s - 1) : C * s], raw[(e, s)][:, 0, H - C : H])
+        scatter(E - 2, 0, turned[:, 0:C], raw[(E - 1, PASSES - 1)][:, 0, H - C : H])
+        last_relu = keep.tile([P, 2, H // 2], F32, name="last_relu")
+        last_pairs = keep.tile([P, 2, C], F32, name="last_pairs")
+        last_turned = [psum.tile([P, C], F32, name="result_bank") for u in range(2)]
+        for u in range(2):
+            activate(E - 1, last_accs[u][:], 1, last_relu[:, u, :], last_turned[u])
+        scatter(E - 2, 1, turned[:, C : 2 * C], last_relu[:, 0, 0:C])
+        for u in range(2):
+            scatter(E - 1, u, last_turned[u][:], last_pairs[:, u, :])
 
-        shares = [(0, SPLIT, nc.vector.tensor_copy), (SPLIT, T, nc.scalar.copy)]
-        planes = [keep.tile([P, 4, b - a], BF16, name="planes_%d" % a) for a, b, copy in shares]
-        for t in range(4):
-            for (a, b, copy), tile in zip(shares, planes):
-                (nc.scalar.copy if t < 3 else copy)(tile[:, t, :], windows[t][:, a:b])
-        bank_names = ["bank_%d" % i for i in range(4)] + ["last_%d" % i for i in range(4)]
-        used = 0
-        for a, halved in CHUNKS:
-            b = a + C
-            first, end, copy = shares[a // SPLIT]
-            c_in = keep.tile([P, b - a, 4], BF16, name="c_in_%d" % a, align_bytes=64)
-            copy(
-                c_in[:].rearrange("p (n i) t -> p n t i", i=4),
-                planes[a // SPLIT][:, :, a - first : b - first].rearrange("p t (n i) -> p n t i", i=4),
-            )
-            c_words = keep.tile([P, b - a], U32, name="c_words_%d" % a, align_bytes=64)
-            c_plane = keep.tile([P, b - a], U8, name="c_plane_%d" % a, align_bytes=64)
+        halves = keep.tile([P, 2, T], F32, name="halves")
+        nc.scalar.copy(halves[:, 0, :], windows[0][:])
+        a = 0
+        for width in TOKEN_CHUNKS:
+            b = a + width
+            (nc.vector.tensor_copy if a == 0 else nc.scalar.copy)(halves[:, 1, a:b], windows[1][:, a:b])
+            c_in = keep.tile([P, width, 2], F32, name="c_in_%d" % a, align_bytes=64)
+            (nc.vector.tensor_copy if a < 512 else nc.scalar.copy)(c_in[:], halves[:, :, a:b].rearrange("p u n -> p n u"))
+            c_words = keep.tile([P, width], U32, name="c_words_%d" % a, align_bytes=64)
+            c_plane = keep.tile([P, width], U8, name="c_plane_%d" % a, align_bytes=64)
             nc.vector.quantize_mx(
-                out=c_words[:].bitcast(FP8X4), scales=c_plane[:], in_=c_in[:].rearrange("p n t -> p (n t)")
+                out=c_words[:].bitcast(FP8X4),
+                scales=c_plane[:],
+                in_=c_in[:].rearrange("p n u -> p (n u)").bitcast(BF16),
             )
-            result = keep.tile([P, 2, b - a], F32, name="result_%d" % a)
-            if halved:
-                accs = [psum.tile([P, C], F32, name=bank_names[(used + h) % 8])[:] for h in range(2)]
-                used += 2
-            else:
-                bank = psum.tile([P, 2, C], F32, name=bank_names[used % 8])
-                accs = [bank[:, h, :] for h in range(2)]
-                used += 1
+            bank = psum.tile([P, 2, width], F32, name="acc" if a < T // 2 else "result_bank")
             for h in range(2):
                 nc.tensor.matmul_mx(
-                    out=accs[h],
+                    out=bank[:, h, :],
                     lhsT=w2_tile[:, P * h : P * (h + 1)].bitcast(FP8X4),
                     lhsT_scale=w2_plane[:].bitcast(U8)[:, P * h : P * (h + 1)],
                     rhs=c_words[:].bitcast(FP8X4),
@@ -219,9 +189,7 @@ def tile_moe_sdn_lin_relu2_kernel(
                     start=True,
                     stop=True,
                 )
-            if halved:
-                nc.scalar.copy(result[:, 0, :], accs[0])
-                nc.vector.tensor_copy(result[:, 1, :], accs[1])
-            else:
-                nc.scalar.copy(result[:], bank[:])
+            result = keep.tile([P, 2, width], F32, name="result_%d" % a)
+            (nc.scalar.copy if b < T else nc.vector.tensor_copy)(result[:], bank[:])
             nc.sync.dma_start(out.rearrange("(h p) t -> p h t", h=2)[:, :, a:b], result[:])
+            a = b

@@ -19,8 +19,8 @@ ALU = mybir.AluOpType
 P = 128
 PASSES = K // 512
 GATHER = 384
-VECTOR_SHARE = 48
-TOKEN_CHUNKS = [256, 256, 128, 128]
+VECTOR_COLUMNS = 160
+TOKEN_CHUNKS = [(0, 128), (128, 384), (384, 640), (640, 768)]
 
 
 def tile_moe_sdn_lin_relu2_kernel(
@@ -85,6 +85,13 @@ def tile_moe_sdn_lin_relu2_kernel(
                 raw[(e, s)][:].rearrange("p j (m u d) -> p m j u d", u=2, d=2)[:, m0:m1, :, u0:u1],
             )
 
+        def cast_plain(e, s, grouped, c0, c1, copy):
+            flat = grouped[:].rearrange("p u m d j -> p (u m d) j")
+            copy(
+                flat[:, c0:c1, :].rearrange("p (c i) j -> p c j i", i=4),
+                raw[(e, s)][:, :, c0:c1].rearrange("p j (c i) -> p c j i", i=4),
+            )
+
         def quantize(grouped, words, plane, u0, u1):
             cols = slice(2 * P * u0, 2 * P * u1)
             nc.vector.quantize_mx(
@@ -109,12 +116,13 @@ def tile_moe_sdn_lin_relu2_kernel(
         windows = [keep.tile([P, T], F32, name="window_%d" % u) for u in range(2)]
 
         def activate(e, acc, halves, relu, turned):
-            nc.scalar.activation(relu, acc, ACT.Relu)
+            sums = acc.rearrange("p (u c) -> p u c", c=C)
+            nc.scalar.activation(relu, sums, ACT.Copy, scale=gate_columns[:, e : e + 1])
             gated = ring.tile([P, 2 * P * halves], BF16, name="gated", bufs=2)
-            nc.vector.scalar_tensor_tensor(gated[:], relu, gate_columns[:, e : e + 1], relu, ALU.mult, ALU.mult)
+            nc.vector.scalar_tensor_tensor(gated[:].rearrange("p (u c) -> p u c", c=C), sums, 0.0, relu, ALU.max, ALU.mult)
             for u in range(halves):
-                cols = slice(P * u, P * (u + 1))
-                nc.tensor.transpose(turned[:, cols], gated[:].bitcast(F32)[:, cols], identity[:])
+                pair_words = gated[:].bitcast(F32)[:, u : P * halves : halves]
+                nc.tensor.transpose(turned[:, P * u : P * (u + 1)], pair_words, identity[:])
 
         def scatter(e, u, turned, pairs):
             nc.scalar.copy(pairs, turned)
@@ -129,20 +137,26 @@ def tile_moe_sdn_lin_relu2_kernel(
                 grouped = ring.tile([P, 2, P, 2, 4], BF16, name="grouped", align_bytes=64)
                 words = ring.tile([P, H], U32, name="w1_words", align_bytes=64)
                 plane = ring.tile([P, H], U8, name="w1_plane", align_bytes=64)
-                split = 64 if (e, s) == (E - 1, 1) else VECTOR_SHARE
                 if (e, s) == (E - 1, PASSES - 1):
-                    cast(e, s, grouped, 0, 1, 0, P, nc.vector.tensor_copy)
-                    cast(e, s, grouped, 1, 2, 0, 32, nc.vector.tensor_copy)
-                    cast(e, s, grouped, 1, 2, 32, P, nc.scalar.copy)
+                    cast(e, s, grouped, 0, 1, 0, 84, nc.vector.tensor_copy)
+                    cast(e, s, grouped, 0, 1, 84, P, nc.scalar.copy)
+                    cast(e, s, grouped, 1, 2, 0, 48, nc.vector.tensor_copy)
+                    cast(e, s, grouped, 1, 2, 48, P, nc.scalar.copy)
                     for u in range(2):
                         quantize(grouped, words, plane, u, u + 1)
-                else:
-                    if e == 0 and s < 2:
-                        split = 0
+                elif e < E - 1:
+                    split = 0 if e == 0 and s < 2 else VECTOR_COLUMNS
                     if split > 0:
-                        cast(e, s, grouped, 0, 2, 0, split, nc.vector.tensor_copy)
-                    cast(e, s, grouped, 0, 2, split, P, nc.scalar.copy)
-                    quantize(grouped, words, plane, 0, 2)
+                        cast_plain(e, s, grouped, 0, split, nc.vector.tensor_copy)
+                    cast_plain(e, s, grouped, split, H, nc.scalar.copy)
+                    for u in (1, 0):
+                        quantize(grouped, words, plane, u, u + 1)
+                else:
+                    cast(e, s, grouped, 0, 1, 0, VECTOR_COLUMNS // 2, nc.vector.tensor_copy)
+                    cast(e, s, grouped, 1, 2, 0, P, nc.scalar.copy)
+                    cast(e, s, grouped, 0, 1, VECTOR_COLUMNS // 2, P, nc.scalar.copy)
+                    for u in (1, 0):
+                        quantize(grouped, words, plane, u, u + 1)
                 if e < E - 1:
                     multiply(e, s, words, plane, 0, 2, acc[:])
                 else:
@@ -150,38 +164,44 @@ def tile_moe_sdn_lin_relu2_kernel(
                         multiply(e, s, words, plane, u, u + 1, last_accs[u][:])
                 if e > 0 and s == 0:
                     turned = psum.tile([P, 2 * C], F32, name="turned")
-                    activate(e - 1, previous[:], 2, raw[(e, s)][:, 0, :], turned)
+                    activate(e - 1, previous[:], 2, raw[(e, s)][:, :, 0:C], turned)
                 if 0 < e < E - 1 and s > 0:
-                    scatter(e - 1, s - 1, turned[:, C * (s - 1) : C * s], raw[(e, s)][:, 0, H - C : H])
-        scatter(E - 2, 0, turned[:, 0:C], raw[(E - 1, PASSES - 1)][:, 0, H - C : H])
+                    scatter(e - 1, s - 1, turned[:, C * (s - 1) : C * s], raw[(e, s)][:, 0, 0:C])
+        scatter(E - 2, 0, turned[:, 0:C], raw[(E - 1, PASSES - 1)][:, 3, H - C : H])
         last_relu = keep.tile([P, 2, H // 2], F32, name="last_relu")
         last_pairs = keep.tile([P, 2, C], F32, name="last_pairs")
         last_turned = [psum.tile([P, C], F32, name="result_bank") for u in range(2)]
         for u in range(2):
-            activate(E - 1, last_accs[u][:], 1, last_relu[:, u, :], last_turned[u])
+            activate(E - 1, last_accs[u][:], 1, last_relu[:, u, :].rearrange("p (u c) -> p u c", c=C), last_turned[u])
         scatter(E - 2, 1, turned[:, C : 2 * C], last_relu[:, 0, 0:C])
         for u in range(2):
             scatter(E - 1, u, last_turned[u][:], last_pairs[:, u, :])
 
         halves = keep.tile([P, 2, T], F32, name="halves")
         nc.scalar.copy(halves[:, 0, :], windows[0][:])
-        a = 0
-        for width in TOKEN_CHUNKS:
-            b = a + width
-            (nc.vector.tensor_copy if a == 0 else nc.scalar.copy)(halves[:, 1, a:b], windows[1][:, a:b])
-            c_in = keep.tile([P, width, 2], F32, name="c_in_%d" % a, align_bytes=64)
-            (nc.vector.tensor_copy if a < 512 else nc.scalar.copy)(c_in[:], halves[:, :, a:b].rearrange("p u n -> p n u"))
-            c_words = keep.tile([P, width], U32, name="c_words_%d" % a, align_bytes=64)
-            c_plane = keep.tile([P, width], U8, name="c_plane_%d" % a, align_bytes=64)
+        nc.scalar.copy(halves[:, 1, T // 2 : T], windows[1][:, T // 2 : T])
+        for a, b in TOKEN_CHUNKS[:2]:
+            nc.vector.tensor_copy(halves[:, 1, a:b], windows[1][:, a:b])
+        c_in = {}
+        for a, b in TOKEN_CHUNKS:
+            c_in[a] = keep.tile([P, b - a, 2], F32, name="c_in_%d" % a, align_bytes=64)
+            copy = nc.vector.tensor_copy if a < T // 2 else nc.scalar.copy
+            copy(c_in[a][:], halves[:, :, a:b].rearrange("p u n -> p n u"))
+        free_banks = ["acc", "acc", "turned", "turned", "result_bank", "result_bank", "last_acc_0", "last_acc_1"]
+        banks = {}
+        for a, b in TOKEN_CHUNKS:
+            c_words = keep.tile([P, b - a], U32, name="c_words_%d" % a, align_bytes=64)
+            c_plane = keep.tile([P, b - a], U8, name="c_plane_%d" % a, align_bytes=64)
             nc.vector.quantize_mx(
                 out=c_words[:].bitcast(FP8X4),
                 scales=c_plane[:],
-                in_=c_in[:].rearrange("p n u -> p (n u)").bitcast(BF16),
+                in_=c_in[a][:].rearrange("p n u -> p (n u)").bitcast(BF16),
             )
-            bank = psum.tile([P, 2, width], F32, name="acc" if a < T // 2 else "result_bank")
             for h in range(2):
+                tag = free_banks[len(banks)]
+                banks[(a, h)] = psum.tile([P, b - a], F32, name=tag, bufs=1 if tag.startswith("last") else 2)
                 nc.tensor.matmul_mx(
-                    out=bank[:, h, :],
+                    out=banks[(a, h)][:],
                     lhsT=w2_tile[:, P * h : P * (h + 1)].bitcast(FP8X4),
                     lhsT_scale=w2_plane[:].bitcast(U8)[:, P * h : P * (h + 1)],
                     rhs=c_words[:].bitcast(FP8X4),
@@ -189,7 +209,8 @@ def tile_moe_sdn_lin_relu2_kernel(
                     start=True,
                     stop=True,
                 )
-            result = keep.tile([P, 2, width], F32, name="result_%d" % a)
-            (nc.scalar.copy if b < T else nc.vector.tensor_copy)(result[:], bank[:])
+        for a, b in TOKEN_CHUNKS:
+            result = keep.tile([P, 2, b - a], F32, name="result_%d" % a)
+            (nc.vector.tensor_copy if a > 0 else nc.scalar.copy)(result[:, 0, :], banks[(a, 0)][:])
+            nc.scalar.copy(result[:, 1, :], banks[(a, 1)][:])
             nc.sync.dma_start(out.rearrange("(h p) t -> p h t", h=2)[:, :, a:b], result[:])
-            a = b

@@ -19,7 +19,7 @@ ALU = mybir.AluOpType
 P = 128
 PASSES = K // 512
 GATHER = 384
-VECTOR_COLUMNS = 160
+VECTOR_COLUMNS = 216
 TOKEN_CHUNKS = [(0, 128), (128, 384), (384, 640), (640, 768)]
 
 
@@ -145,7 +145,7 @@ def tile_moe_sdn_lin_relu2_kernel(
                     for u in range(2):
                         quantize(grouped, words, plane, u, u + 1)
                 elif e < E - 1:
-                    split = 0 if e == 0 and s < 2 else VECTOR_COLUMNS
+                    split = (0, 0, H // 2)[s] if e == 0 else VECTOR_COLUMNS
                     if split > 0:
                         cast_plain(e, s, grouped, 0, split, nc.vector.tensor_copy)
                     cast_plain(e, s, grouped, split, H, nc.scalar.copy)
@@ -210,7 +210,7 @@ def tile_moe_sdn_lin_relu2_kernel(
                     stop=True,
                 )
         for a, b in TOKEN_CHUNKS:
-            result = keep.tile([P, 2, b - a], F32, name="result_%d" % a)
-            (nc.vector.tensor_copy if a > 0 else nc.scalar.copy)(result[:, 0, :], banks[(a, 0)][:])
-            nc.scalar.copy(result[:, 1, :], banks[(a, 1)][:])
-            nc.sync.dma_start(out.rearrange("(h p) t -> p h t", h=2)[:, :, a:b], result[:])
+            for h in range(2):
+                result = keep.tile([P, b - a], F32, name="result_%d_%d" % (a, h))
+                (nc.vector.tensor_copy if a > 0 and h == 0 else nc.scalar.copy)(result[:], banks[(a, h)][:])
+                nc.sync.dma_start(out[P * h : P * (h + 1), a:b], result[:])

@@ -18,8 +18,10 @@ ALU = mybir.AluOpType
 
 P = 128
 PASSES = K // 512
-GATHER = 384
-VECTOR_COLUMNS = 216
+LAST = E - 1
+GATHER = T // 2
+VECTOR_COLUMNS = 200
+LAST_VECTOR_GROUPS = (84, 48)
 TOKEN_CHUNKS = [(0, 128), (128, 384), (384, 640), (640, 768)]
 
 
@@ -58,7 +60,7 @@ def tile_moe_sdn_lin_relu2_kernel(
                         nc.sync.dma_start(
                             x_plane[32 * q : 32 * q + 4 * PASSES, :], x_scales[:, 4 * q : 4 * q + 4, :].bitcast(I32)
                         )
-                if (e, s) == (0, 2):
+                if (e, s) == (0, PASSES - 1):
                     nc.sync.dma_start(gate_rows[0:E, :], gate[0].rearrange("(e c) -> e c", e=E))
         nc.sync.dma_start(w2_tile[:], w2_words[0].rearrange("p n d -> p (n d)").bitcast(I32))
         for q in range(4):
@@ -68,126 +70,125 @@ def tile_moe_sdn_lin_relu2_kernel(
         slot_plane = keep.tile([P, T], U8, name="slot_plane", align_bytes=64)
         for s in range(PASSES):
             for a in range(0, T, GATHER):
-                lst = offsets[:, a // 16 : (a + GATHER) // 16]
-                nc.vector.tensor_copy(slot_words[:, s, a : a + GATHER], x_tile[:, s, :].bitcast(U32).indirect(lst))
+                entries = offsets[:, a // 16 : (a + GATHER) // 16]
+                nc.vector.tensor_copy(slot_words[:, s, a : a + GATHER], x_tile[:, s, :].bitcast(U32).indirect(entries))
         for a in range(0, T, GATHER):
-            lst = offsets[:, a // 16 : (a + GATHER) // 16]
-            nc.vector.tensor_copy(slot_plane[:, a : a + GATHER], x_plane[:].bitcast(U8).indirect(lst))
+            entries = offsets[:, a // 16 : (a + GATHER) // 16]
+            nc.vector.tensor_copy(slot_plane[:, a : a + GATHER], x_plane[:].bitcast(U8).indirect(entries))
 
-        gate_bank = psum.tile([P, 2, C], F32, name="turned")
-        nc.tensor.transpose(gate_bank[:, 0, :], gate_rows[:], identity[:])
-        gate_columns = keep.tile([P, 8], F32, name="gate_columns")
-        nc.scalar.copy(gate_columns[:], gate_bank[:, 0, 0:8])
+        gate_bank = psum.tile([P, P], F32, name="turned")
+        nc.tensor.transpose(gate_bank[:], gate_rows[:], identity[:])
+        gate_columns = keep.tile([P, E], F32, name="gate_columns")
+        nc.scalar.copy(gate_columns[:], gate_bank[:, 0:E])
 
-        def cast(e, s, grouped, u0, u1, m0, m1, copy):
+        def round_columns(e, s, grouped, c0, c1, copy):
             copy(
-                grouped[:, u0:u1, m0:m1].rearrange("p u m d j -> p m j u d"),
-                raw[(e, s)][:].rearrange("p j (m u d) -> p m j u d", u=2, d=2)[:, m0:m1, :, u0:u1],
-            )
-
-        def cast_plain(e, s, grouped, c0, c1, copy):
-            flat = grouped[:].rearrange("p u m d j -> p (u m d) j")
-            copy(
-                flat[:, c0:c1, :].rearrange("p (c i) j -> p c j i", i=4),
+                grouped[:, c0:c1, :].rearrange("p (c i) j -> p c j i", i=4),
                 raw[(e, s)][:, :, c0:c1].rearrange("p j (c i) -> p c j i", i=4),
             )
 
-        def quantize(grouped, words, plane, u0, u1):
-            cols = slice(2 * P * u0, 2 * P * u1)
-            nc.vector.quantize_mx(
-                out=words[:, cols].bitcast(FP8X4),
-                scales=plane[:, cols],
-                in_=grouped[:, u0:u1].rearrange("p u m d j -> p (u m d j)"),
+        def round_half(e, s, grouped, u, m0, m1, copy):
+            copy(
+                grouped[:].rearrange("p (u m d) j -> p u m j d", u=2, d=2)[:, u, m0:m1],
+                raw[(e, s)][:].rearrange("p j (m u d) -> p u m j d", u=2, d=2)[:, u, m0:m1],
             )
 
-        def multiply(e, s, words, plane, u0, u1, acc):
+        def quantize(grouped, words, plane, c0, c1):
+            nc.vector.quantize_mx(
+                out=words[:, c0:c1].bitcast(FP8X4),
+                scales=plane[:, c0:c1],
+                in_=grouped[:, c0:c1, :].rearrange("p c j -> p (c j)"),
+            )
+
+        def first_product(e, s, words, plane, c0, c1, sums):
             slots = slice(C * e, C * (e + 1))
-            cols = slice(2 * P * u0, 2 * P * u1)
             nc.tensor.matmul_mx(
-                out=acc,
+                out=sums,
                 lhsT=slot_words[:, s, slots].bitcast(FP8X4),
                 lhsT_scale=slot_plane[4 * s : P, slots],
-                rhs=words[:, cols].bitcast(FP8X4),
-                rhs_scale=plane[:, cols],
+                rhs=words[:, c0:c1].bitcast(FP8X4),
+                rhs_scale=plane[:, c0:c1],
                 start=(s == 0),
                 stop=(s == PASSES - 1),
             )
 
         windows = [keep.tile([P, T], F32, name="window_%d" % u) for u in range(2)]
 
-        def activate(e, acc, halves, relu, turned):
-            sums = acc.rearrange("p (u c) -> p u c", c=C)
-            nc.scalar.activation(relu, sums, ACT.Copy, scale=gate_columns[:, e : e + 1])
+        def gate_and_turn(e, sums, halves, scaled, turned):
+            rows = sums.rearrange("p (r c) -> p r c", c=C)
+            nc.scalar.activation(scaled, rows, ACT.Copy, scale=gate_columns[:, e : e + 1])
             gated = ring.tile([P, 2 * P * halves], BF16, name="gated", bufs=2)
-            nc.vector.scalar_tensor_tensor(gated[:].rearrange("p (u c) -> p u c", c=C), sums, 0.0, relu, ALU.max, ALU.mult)
+            nc.vector.scalar_tensor_tensor(
+                gated[:].rearrange("p (r c) -> p r c", c=C), rows, 0.0, scaled, ALU.max, ALU.mult
+            )
             for u in range(halves):
                 pair_words = gated[:].bitcast(F32)[:, u : P * halves : halves]
                 nc.tensor.transpose(turned[:, P * u : P * (u + 1)], pair_words, identity[:])
 
-        def scatter(e, u, turned, pairs):
-            nc.scalar.copy(pairs, turned)
+        def scatter(e, u, turned_half, pairs):
+            nc.scalar.copy(pairs, turned_half)
             nc.vector.tensor_copy(windows[u][:].indirect(offsets[:, C * e // 16 : C * (e + 1) // 16]), pairs)
 
-        last_accs = [psum.tile([P, H // 2], F32, name="last_acc_%d" % u, bufs=1) for u in range(2)]
+        half_width = H // 2
+        last_sums = [psum.tile([P, half_width], F32, name="last_sums_%d" % u, bufs=1) for u in range(2)]
+        sums = {}
         for e in range(E):
-            previous = acc if e > 0 else None
-            if e < E - 1:
-                acc = psum.tile([P, H], F32, name="acc")
+            if e < LAST:
+                sums[e] = psum.tile([P, H], F32, name="sums")
             for s in range(PASSES):
-                grouped = ring.tile([P, 2, P, 2, 4], BF16, name="grouped", align_bytes=64)
+                grouped = ring.tile([P, H, 4], BF16, name="grouped", align_bytes=64)
                 words = ring.tile([P, H], U32, name="w1_words", align_bytes=64)
                 plane = ring.tile([P, H], U8, name="w1_plane", align_bytes=64)
-                if (e, s) == (E - 1, PASSES - 1):
-                    cast(e, s, grouped, 0, 1, 0, 84, nc.vector.tensor_copy)
-                    cast(e, s, grouped, 0, 1, 84, P, nc.scalar.copy)
-                    cast(e, s, grouped, 1, 2, 0, 48, nc.vector.tensor_copy)
-                    cast(e, s, grouped, 1, 2, 48, P, nc.scalar.copy)
-                    for u in range(2):
-                        quantize(grouped, words, plane, u, u + 1)
-                elif e < E - 1:
-                    split = (0, 0, H // 2)[s] if e == 0 else VECTOR_COLUMNS
+                if e < LAST:
+                    split = (0, 0, half_width)[s] if e == 0 else VECTOR_COLUMNS
                     if split > 0:
-                        cast_plain(e, s, grouped, 0, split, nc.vector.tensor_copy)
-                    cast_plain(e, s, grouped, split, H, nc.scalar.copy)
-                    for u in (1, 0):
-                        quantize(grouped, words, plane, u, u + 1)
-                else:
-                    cast(e, s, grouped, 0, 1, 0, VECTOR_COLUMNS // 2, nc.vector.tensor_copy)
-                    cast(e, s, grouped, 1, 2, 0, P, nc.scalar.copy)
-                    cast(e, s, grouped, 0, 1, VECTOR_COLUMNS // 2, P, nc.scalar.copy)
-                    for u in (1, 0):
-                        quantize(grouped, words, plane, u, u + 1)
-                if e < E - 1:
-                    multiply(e, s, words, plane, 0, 2, acc[:])
+                        round_columns(e, s, grouped, 0, split, nc.vector.tensor_copy)
+                    round_columns(e, s, grouped, split, H, nc.scalar.copy)
+                elif s < PASSES - 1:
+                    round_half(e, s, grouped, 0, 0, VECTOR_COLUMNS // 2, nc.vector.tensor_copy)
+                    round_half(e, s, grouped, 1, 0, P, nc.scalar.copy)
+                    round_half(e, s, grouped, 0, VECTOR_COLUMNS // 2, P, nc.scalar.copy)
                 else:
                     for u in range(2):
-                        multiply(e, s, words, plane, u, u + 1, last_accs[u][:])
+                        round_half(e, s, grouped, u, 0, LAST_VECTOR_GROUPS[u], nc.vector.tensor_copy)
+                        round_half(e, s, grouped, u, LAST_VECTOR_GROUPS[u], P, nc.scalar.copy)
+                for c0 in (0, half_width) if (e, s) == (LAST, PASSES - 1) else (half_width, 0):
+                    quantize(grouped, words, plane, c0, c0 + half_width)
+                if e < LAST:
+                    first_product(e, s, words, plane, 0, H, sums[e][:])
+                else:
+                    for u in range(2):
+                        first_product(e, s, words, plane, half_width * u, half_width * (u + 1), last_sums[u][:])
                 if e > 0 and s == 0:
                     turned = psum.tile([P, 2 * C], F32, name="turned")
-                    activate(e - 1, previous[:], 2, raw[(e, s)][:, :, 0:C], turned)
-                if 0 < e < E - 1 and s > 0:
+                    gate_and_turn(e - 1, sums[e - 1][:], 2, raw[(e, s)][:, :, 0:C], turned)
+                if 0 < e < LAST and s > 0:
                     scatter(e - 1, s - 1, turned[:, C * (s - 1) : C * s], raw[(e, s)][:, 0, 0:C])
-        scatter(E - 2, 0, turned[:, 0:C], raw[(E - 1, PASSES - 1)][:, 3, H - C : H])
-        last_relu = keep.tile([P, 2, H // 2], F32, name="last_relu")
-        last_pairs = keep.tile([P, 2, C], F32, name="last_pairs")
-        last_turned = [psum.tile([P, C], F32, name="result_bank") for u in range(2)]
-        for u in range(2):
-            activate(E - 1, last_accs[u][:], 1, last_relu[:, u, :].rearrange("p (u c) -> p u c", c=C), last_turned[u])
-        scatter(E - 2, 1, turned[:, C : 2 * C], last_relu[:, 0, 0:C])
-        for u in range(2):
-            scatter(E - 1, u, last_turned[u][:], last_pairs[:, u, :])
 
-        halves = keep.tile([P, 2, T], F32, name="halves")
-        nc.scalar.copy(halves[:, 0, :], windows[0][:])
-        nc.scalar.copy(halves[:, 1, T // 2 : T], windows[1][:, T // 2 : T])
+        scatter(LAST - 1, 0, turned[:, 0:C], raw[(LAST, PASSES - 1)][:, 3, H - C : H])
+        last_scaled = keep.tile([P, 2, half_width], F32, name="last_scaled")
+        last_pairs = keep.tile([P, 2, C], F32, name="last_pairs")
+        last_turned = [psum.tile([P, C], F32, name="last_turned") for u in range(2)]
+        for u in range(2):
+            scaled = last_scaled[:, u, :].rearrange("p (r c) -> p r c", c=C)
+            gate_and_turn(LAST, last_sums[u][:], 1, scaled, last_turned[u])
+        scatter(LAST - 1, 1, turned[:, C : 2 * C], last_scaled[:, 0, 0:C])
+        for u in range(2):
+            scatter(LAST, u, last_turned[u][:], last_pairs[:, u, :])
+
+        both = keep.tile([P, 2, T], F32, name="both")
+        nc.scalar.copy(both[:, 0, :], windows[0][:])
+        nc.scalar.copy(both[:, 1, T // 2 : T], windows[1][:, T // 2 : T])
         for a, b in TOKEN_CHUNKS[:2]:
-            nc.vector.tensor_copy(halves[:, 1, a:b], windows[1][:, a:b])
+            nc.vector.tensor_copy(both[:, 1, a:b], windows[1][:, a:b])
         c_in = {}
         for a, b in TOKEN_CHUNKS:
             c_in[a] = keep.tile([P, b - a, 2], F32, name="c_in_%d" % a, align_bytes=64)
-            copy = nc.vector.tensor_copy if a < T // 2 else nc.scalar.copy
-            copy(c_in[a][:], halves[:, :, a:b].rearrange("p u n -> p n u"))
-        free_banks = ["acc", "acc", "turned", "turned", "result_bank", "result_bank", "last_acc_0", "last_acc_1"]
+            interleave = nc.vector.tensor_copy if a < T // 2 else nc.scalar.copy
+            interleave(c_in[a][:], both[:, :, a:b].rearrange("p u n -> p n u"))
+
+        bank_tags = [("sums", 2)] * 2 + [("turned", 2)] * 2 + [("last_turned", 2)] * 2
+        bank_tags = bank_tags + [("last_sums_0", 1), ("last_sums_1", 1)]
         banks = {}
         for a, b in TOKEN_CHUNKS:
             c_words = keep.tile([P, b - a], U32, name="c_words_%d" % a, align_bytes=64)
@@ -198,8 +199,8 @@ def tile_moe_sdn_lin_relu2_kernel(
                 in_=c_in[a][:].rearrange("p n u -> p (n u)").bitcast(BF16),
             )
             for h in range(2):
-                tag = free_banks[len(banks)]
-                banks[(a, h)] = psum.tile([P, b - a], F32, name=tag, bufs=1 if tag.startswith("last") else 2)
+                tag, bufs = bank_tags[len(banks)]
+                banks[(a, h)] = psum.tile([P, b - a], F32, name=tag, bufs=bufs)
                 nc.tensor.matmul_mx(
                     out=banks[(a, h)][:],
                     lhsT=w2_tile[:, P * h : P * (h + 1)].bitcast(FP8X4),
@@ -212,5 +213,6 @@ def tile_moe_sdn_lin_relu2_kernel(
         for a, b in TOKEN_CHUNKS:
             for h in range(2):
                 result = keep.tile([P, b - a], F32, name="result_%d_%d" % (a, h))
-                (nc.vector.tensor_copy if a > 0 and h == 0 else nc.scalar.copy)(result[:], banks[(a, h)][:])
+                empty = nc.vector.tensor_copy if a > 0 and h == 0 else nc.scalar.copy
+                empty(result[:], banks[(a, h)][:])
                 nc.sync.dma_start(out[P * h : P * (h + 1), a:b], result[:])

@@ -21,7 +21,8 @@ PASSES = K // 512
 LAST = E - 1
 GATHER = T // 2
 VECTOR_COLUMNS = 200
-LAST_VECTOR_GROUPS = (84, 48)
+SIDE_GROUPS = (42, 42, 42)
+LG = (50, 50)
 TOKEN_CHUNKS = [(0, 128), (128, 384), (384, 640), (640, 768)]
 
 
@@ -53,8 +54,15 @@ def tile_moe_sdn_lin_relu2_kernel(
         raw = {}
         for e in range(E):
             for s in range(PASSES):
+                rows = w1[e, 512 * s : 512 * (s + 1), :].rearrange("(p j) c -> p j c", j=4)
+                if (e, s) == (LAST, PASSES - 1):
+                    raw_sides = []
+                    for side in range(2):
+                        raw_sides.append(keep.tile([P, 4, H // 2], F32, name="raw_side_%d" % side))
+                        nc.sync.dma_start(raw_sides[side][:], rows[:, :, H // 2 * side : H // 2 * (side + 1)])
+                    continue
                 raw[(e, s)] = keep.tile([P, 4, H], F32, name="raw_%d_%d" % (e, s))
-                nc.sync.dma_start(raw[(e, s)][:], w1[e, 512 * s : 512 * (s + 1), :].rearrange("(p j) c -> p j c", j=4))
+                nc.sync.dma_start(raw[(e, s)][:], rows)
                 if (e, s) == (0, 0):
                     for q in range(4):
                         nc.sync.dma_start(
@@ -87,17 +95,19 @@ def tile_moe_sdn_lin_relu2_kernel(
                 raw[(e, s)][:, :, c0:c1].rearrange("p j (c i) -> p c j i", i=4),
             )
 
-        def round_half(e, s, grouped, u, m0, m1, copy):
-            copy(
-                grouped[:].rearrange("p (u m d) j -> p u m j d", u=2, d=2)[:, u, m0:m1],
-                raw[(e, s)][:].rearrange("p j (m u d) -> p u m j d", u=2, d=2)[:, u, m0:m1],
-            )
+        def round_side(source, grouped, side, u, m0, m1, copy):
+            columns = source.rearrange("p j (m u d) -> p m j u d", u=2, d=2)
+            if u is None:
+                places = grouped[:, H // 2 * side : H // 2 * (side + 1), :]
+                copy(places.rearrange("p (u m d) j -> p m j u d", u=2, d=2)[:, m0:m1], columns[:, m0:m1])
+            else:
+                copy(grouped.rearrange("p (m d) j -> p m j d", d=2)[:, m0:m1], columns[:, m0:m1, :, u])
 
         def quantize(grouped, words, plane, c0, c1):
             nc.vector.quantize_mx(
                 out=words[:, c0:c1].bitcast(FP8X4),
                 scales=plane[:, c0:c1],
-                in_=grouped[:, c0:c1, :].rearrange("p c j -> p (c j)"),
+                in_=grouped.rearrange("p c j -> p (c j)"),
             )
 
         def first_product(e, s, words, plane, c0, c1, sums):
@@ -112,25 +122,19 @@ def tile_moe_sdn_lin_relu2_kernel(
                 stop=(s == PASSES - 1),
             )
 
-        windows = [keep.tile([P, T], F32, name="window_%d" % u) for u in range(2)]
+        windows = [keep.tile([P, T + C * (2 - u)], F32, name="window_%d" % u, align_bytes=64) for u in range(2)]
 
-        def gate_and_turn(e, sums, halves, scaled, turned):
-            rows = sums.rearrange("p (r c) -> p r c", c=C)
-            nc.scalar.activation(scaled, rows, ACT.Copy, scale=gate_columns[:, e : e + 1])
-            gated = ring.tile([P, 2 * P * halves], BF16, name="gated", bufs=2)
-            nc.vector.scalar_tensor_tensor(
-                gated[:].rearrange("p (r c) -> p r c", c=C), rows, 0.0, scaled, ALU.max, ALU.mult
-            )
-            for u in range(halves):
-                pair_words = gated[:].bitcast(F32)[:, u : P * halves : halves]
-                nc.tensor.transpose(turned[:, P * u : P * (u + 1)], pair_words, identity[:])
+        def gate_product(e, sums, scaled, gated):
+            nc.scalar.activation(scaled, sums, ACT.Copy, scale=gate_columns[:, e : e + 1])
+            nc.vector.scalar_tensor_tensor(gated, sums, 0.0, scaled, ALU.max, ALU.mult)
 
         def scatter(e, u, turned_half, pairs):
             nc.scalar.copy(pairs, turned_half)
             nc.vector.tensor_copy(windows[u][:].indirect(offsets[:, C * e // 16 : C * (e + 1) // 16]), pairs)
 
         half_width = H // 2
-        last_sums = [psum.tile([P, half_width], F32, name="last_sums_%d" % u, bufs=1) for u in range(2)]
+        last_pieces = [(0, 2 * P), (2 * P, 3 * P), (3 * P, 4 * P)]
+        last_sums = [psum.tile([P, c1 - c0], F32, name="last_sums_%d" % c0, bufs=1) for c0, c1 in last_pieces]
         sums = {}
         for e in range(E):
             if e < LAST:
@@ -139,45 +143,72 @@ def tile_moe_sdn_lin_relu2_kernel(
                 grouped = ring.tile([P, H, 4], BF16, name="grouped", align_bytes=64)
                 words = ring.tile([P, H], U32, name="w1_words", align_bytes=64)
                 plane = ring.tile([P, H], U8, name="w1_plane", align_bytes=64)
+                pieces = [(half_width, H), (0, half_width)]
                 if e < LAST:
                     split = (0, 0, half_width)[s] if e == 0 else VECTOR_COLUMNS
                     if split > 0:
                         round_columns(e, s, grouped, 0, split, nc.vector.tensor_copy)
                     round_columns(e, s, grouped, split, H, nc.scalar.copy)
                 elif s < PASSES - 1:
-                    round_half(e, s, grouped, 0, 0, VECTOR_COLUMNS // 2, nc.vector.tensor_copy)
-                    round_half(e, s, grouped, 1, 0, P, nc.scalar.copy)
-                    round_half(e, s, grouped, 0, VECTOR_COLUMNS // 2, P, nc.scalar.copy)
+                    lower, upper = raw[(e, s)][:, :, 0:half_width], raw[(e, s)][:, :, half_width:H]
+                    round_side(lower, grouped, 0, None, 0, LG[s], nc.vector.tensor_copy)
+                    round_side(upper, grouped, 1, None, 0, P // 2, nc.scalar.copy)
+                    if LG[s] < P // 2:
+                        round_side(lower, grouped, 0, None, LG[s], P // 2, nc.scalar.copy)
                 else:
+                    round_side(raw_sides[0][:], grouped, 0, None, 0, SIDE_GROUPS[0], nc.vector.tensor_copy)
+                    round_side(raw_sides[0][:], grouped, 0, None, SIDE_GROUPS[0], P // 2, nc.scalar.copy)
+                    spare = windows[0][:, T : T + 2 * C].bitcast(BF16).rearrange("p (c j) -> p c j", j=4)
+                    rooms = [grouped[:, 0 : 2 * P, :], spare, grouped[:, 3 * P : 4 * P, :]]
                     for u in range(2):
-                        round_half(e, s, grouped, u, 0, LAST_VECTOR_GROUPS[u], nc.vector.tensor_copy)
-                        round_half(e, s, grouped, u, LAST_VECTOR_GROUPS[u], P, nc.scalar.copy)
-                for c0 in (0, half_width) if (e, s) == (LAST, PASSES - 1) else (half_width, 0):
-                    quantize(grouped, words, plane, c0, c0 + half_width)
+                        round_side(raw_sides[1][:], rooms[1 + u], 1, u, 0, SIDE_GROUPS[1 + u], nc.vector.tensor_copy)
+                        round_side(raw_sides[1][:], rooms[1 + u], 1, u, SIDE_GROUPS[1 + u], P // 2, nc.scalar.copy)
+                    pieces = last_pieces
+                if pieces != last_pieces:
+                    rooms = [grouped[:, c0:c1, :] for c0, c1 in pieces]
+                for (c0, c1), room in zip(pieces, rooms):
+                    quantize(room, words, plane, c0, c1)
                 if e < LAST:
                     first_product(e, s, words, plane, 0, H, sums[e][:])
                 else:
-                    for u in range(2):
-                        first_product(e, s, words, plane, half_width * u, half_width * (u + 1), last_sums[u][:])
+                    for (c0, c1), bank in zip(last_pieces, last_sums):
+                        first_product(e, s, words, plane, c0, c1, bank[:])
                 if e > 0 and s == 0:
                     turned = psum.tile([P, 2 * C], F32, name="turned")
-                    gate_and_turn(e - 1, sums[e - 1][:], 2, raw[(e, s)][:, :, 0:C], turned)
+                    gated = ring.tile([P, H], BF16, name="gated", bufs=2)
+                    gate_product(
+                        e - 1,
+                        sums[e - 1][:].rearrange("p (r c) -> p r c", c=C),
+                        raw[(e, s)][:, :, 0:C] if e < LAST else raw[(e, s)][:, :, H - C : H],
+                        gated[:].rearrange("p (r c) -> p r c", c=C),
+                    )
+                    for u in range(2):
+                        nc.tensor.transpose(turned[:, P * u : P * (u + 1)], gated[:].bitcast(F32)[:, u : 2 * P : 2], identity[:])
                 if 0 < e < LAST and s > 0:
                     scatter(e - 1, s - 1, turned[:, C * (s - 1) : C * s], raw[(e, s)][:, 0, 0:C])
 
-        scatter(LAST - 1, 0, turned[:, 0:C], raw[(LAST, PASSES - 1)][:, 3, H - C : H])
-        last_scaled = keep.tile([P, 2, half_width], F32, name="last_scaled")
+        early_pairs = keep.tile([P, 2 * C], F32, name="early_pairs")
+        nc.scalar.copy(early_pairs[:], turned[:])
+        entries = offsets[:, C * (LAST - 1) // 16 : C * LAST // 16]
+        nc.vector.tensor_copy(windows[0][:].indirect(entries), early_pairs[:, 0:C])
+        last_gated = keep.tile([P, 2, 2, C], BF16, name="last_gated")
+        last_scaled = keep.tile([P, 3, C], F32, name="last_scaled")
         last_pairs = keep.tile([P, 2, C], F32, name="last_pairs")
-        last_turned = [psum.tile([P, C], F32, name="last_turned") for u in range(2)]
+        last_turned = [psum.tile([P, C], F32, name="sums"), psum.tile([P, C], F32, name="last_turned", bufs=1)]
+        gate_product(
+            LAST, last_sums[0][:].rearrange("p (u c) -> p u c", u=2), last_scaled[:, 0:2, :], last_gated[:, :, 0, :]
+        )
+        gate_product(LAST, last_sums[1][:], windows[1][:, T : T + C], last_gated[:, 0, 1, :])
+        gate_product(LAST, last_sums[2][:], last_scaled[:, 2, :], last_gated[:, 1, 1, :])
         for u in range(2):
-            scaled = last_scaled[:, u, :].rearrange("p (r c) -> p r c", c=C)
-            gate_and_turn(LAST, last_sums[u][:], 1, scaled, last_turned[u])
-        scatter(LAST - 1, 1, turned[:, C : 2 * C], last_scaled[:, 0, 0:C])
+            pair_words = last_gated[:, u].rearrange("p s c -> p (s c)").bitcast(F32)
+            nc.tensor.transpose(last_turned[u][:], pair_words, identity[:])
+        nc.vector.tensor_copy(windows[1][:].indirect(entries), early_pairs[:, C : 2 * C])
         for u in range(2):
             scatter(LAST, u, last_turned[u][:], last_pairs[:, u, :])
 
         both = keep.tile([P, 2, T], F32, name="both")
-        nc.scalar.copy(both[:, 0, :], windows[0][:])
+        nc.scalar.copy(both[:, 0, :], windows[0][:, 0:T])
         nc.scalar.copy(both[:, 1, T // 2 : T], windows[1][:, T // 2 : T])
         for a, b in TOKEN_CHUNKS[:2]:
             nc.vector.tensor_copy(both[:, 1, a:b], windows[1][:, a:b])
@@ -187,8 +218,8 @@ def tile_moe_sdn_lin_relu2_kernel(
             interleave = nc.vector.tensor_copy if a < T // 2 else nc.scalar.copy
             interleave(c_in[a][:], both[:, :, a:b].rearrange("p u n -> p n u"))
 
-        bank_tags = [("sums", 2)] * 2 + [("turned", 2)] * 2 + [("last_turned", 2)] * 2
-        bank_tags = bank_tags + [("last_sums_0", 1), ("last_sums_1", 1)]
+        bank_tags = [("last_sums_%d" % c0, 1) for c0, c1 in last_pieces] + [("last_turned", 1)]
+        bank_tags = bank_tags + [("sums", 2)] * 2 + [("turned", 2)] * 2
         banks = {}
         for a, b in TOKEN_CHUNKS:
             c_words = keep.tile([P, b - a], U32, name="c_words_%d" % a, align_bytes=64)

@@ -19,10 +19,11 @@ ALU = mybir.AluOpType
 P = 128
 PASSES = K // 512
 LAST = E - 1
+SIDE = H // 2
 GATHER = T // 2
 VECTOR_COLUMNS = 200
-SIDE_GROUPS = (42, 42, 42)
-LG = (50, 50)
+VECTOR_SIDE_GROUPS = 42
+LAST_PIECES = [(0, SIDE), (SIDE, SIDE + C), (SIDE + C, H)]
 TOKEN_CHUNKS = [(0, 128), (128, 384), (384, 640), (640, 768)]
 
 
@@ -49,20 +50,19 @@ def tile_moe_sdn_lin_relu2_kernel(
 
         x_tile = keep.tile([P, PASSES, T], I32, name="x_tile", align_bytes=64)
         w2_tile = keep.tile([P, N], I32, name="w2_tile", align_bytes=64)
-        for s in range(PASSES):
-            nc.sync.dma_start(x_tile[:, s, :], x_words[s].rearrange("p t d -> p (t d)").bitcast(I32))
+        nc.sync.dma_start(x_tile[:, 0, :], x_words[0].rearrange("p t d -> p (t d)").bitcast(I32))
+        nc.sync.dma_start(x_tile[:, 1:PASSES, :], x_words[1:PASSES].rearrange("s p t d -> p s (t d)").bitcast(I32))
         raw = {}
+        raw_sides = [keep.tile([P, 4, SIDE], F32, name="raw_side_%d" % side) for side in range(2)]
         for e in range(E):
             for s in range(PASSES):
                 rows = w1[e, 512 * s : 512 * (s + 1), :].rearrange("(p j) c -> p j c", j=4)
                 if (e, s) == (LAST, PASSES - 1):
-                    raw_sides = []
                     for side in range(2):
-                        raw_sides.append(keep.tile([P, 4, H // 2], F32, name="raw_side_%d" % side))
-                        nc.sync.dma_start(raw_sides[side][:], rows[:, :, H // 2 * side : H // 2 * (side + 1)])
-                    continue
-                raw[(e, s)] = keep.tile([P, 4, H], F32, name="raw_%d_%d" % (e, s))
-                nc.sync.dma_start(raw[(e, s)][:], rows)
+                        nc.sync.dma_start(raw_sides[side][:], rows[:, :, SIDE * side : SIDE * (side + 1)])
+                else:
+                    raw[(e, s)] = keep.tile([P, 4, H], F32, name="raw_%d_%d" % (e, s))
+                    nc.sync.dma_start(raw[(e, s)][:], rows)
                 if (e, s) == (0, 0):
                     for q in range(4):
                         nc.sync.dma_start(
@@ -89,25 +89,16 @@ def tile_moe_sdn_lin_relu2_kernel(
         gate_columns = keep.tile([P, E], F32, name="gate_columns")
         nc.scalar.copy(gate_columns[:], gate_bank[:, 0:E])
 
-        def round_columns(e, s, grouped, c0, c1, copy):
+        def round_columns(source, grouped, c0, c1, copy):
             copy(
                 grouped[:, c0:c1, :].rearrange("p (c i) j -> p c j i", i=4),
-                raw[(e, s)][:, :, c0:c1].rearrange("p j (c i) -> p c j i", i=4),
+                source[:, :, c0:c1].rearrange("p j (c i) -> p c j i", i=4),
             )
 
-        def round_side(source, grouped, side, u, m0, m1, copy):
-            columns = source.rearrange("p j (m u d) -> p m j u d", u=2, d=2)
-            if u is None:
-                places = grouped[:, H // 2 * side : H // 2 * (side + 1), :]
-                copy(places.rearrange("p (u m d) j -> p m j u d", u=2, d=2)[:, m0:m1], columns[:, m0:m1])
-            else:
-                copy(grouped.rearrange("p (m d) j -> p m j d", d=2)[:, m0:m1], columns[:, m0:m1, :, u])
-
-        def quantize(grouped, words, plane, c0, c1):
-            nc.vector.quantize_mx(
-                out=words[:, c0:c1].bitcast(FP8X4),
-                scales=plane[:, c0:c1],
-                in_=grouped.rearrange("p c j -> p (c j)"),
+        def round_half(side, u, room, m0, m1, copy):
+            copy(
+                room.rearrange("p (m d) j -> p m j d", d=2)[:, m0:m1],
+                side.rearrange("p j (m u d) -> p u m j d", u=2, d=2)[:, u, m0:m1],
             )
 
         def first_product(e, s, words, plane, c0, c1, sums):
@@ -122,19 +113,20 @@ def tile_moe_sdn_lin_relu2_kernel(
                 stop=(s == PASSES - 1),
             )
 
-        windows = [keep.tile([P, T + C * (2 - u)], F32, name="window_%d" % u, align_bytes=64) for u in range(2)]
-
-        def gate_product(e, sums, scaled, gated):
+        def scale_by_gate(e, sums, scaled):
             nc.scalar.activation(scaled, sums, ACT.Copy, scale=gate_columns[:, e : e + 1])
+
+        def gate_product(sums, scaled, gated):
             nc.vector.scalar_tensor_tensor(gated, sums, 0.0, scaled, ALU.max, ALU.mult)
 
-        def scatter(e, u, turned_half, pairs):
-            nc.scalar.copy(pairs, turned_half)
+        windows = [keep.tile([P, T + C * (2 - u)], F32, name="window_%d" % u, align_bytes=64) for u in range(2)]
+        half_0_room = windows[0][:, T : T + 2 * C].bitcast(BF16).rearrange("p (c j) -> p c j", j=4)
+        half_0_scaled = windows[1][:, T : T + C]
+
+        def scatter(e, u, pairs):
             nc.vector.tensor_copy(windows[u][:].indirect(offsets[:, C * e // 16 : C * (e + 1) // 16]), pairs)
 
-        half_width = H // 2
-        last_pieces = [(0, 2 * P), (2 * P, 3 * P), (3 * P, 4 * P)]
-        last_sums = [psum.tile([P, c1 - c0], F32, name="last_sums_%d" % c0, bufs=1) for c0, c1 in last_pieces]
+        last_sums = [psum.tile([P, c1 - c0], F32, name="last_sums_%d" % c0, bufs=1) for c0, c1 in LAST_PIECES]
         sums = {}
         for e in range(E):
             if e < LAST:
@@ -143,69 +135,80 @@ def tile_moe_sdn_lin_relu2_kernel(
                 grouped = ring.tile([P, H, 4], BF16, name="grouped", align_bytes=64)
                 words = ring.tile([P, H], U32, name="w1_words", align_bytes=64)
                 plane = ring.tile([P, H], U8, name="w1_plane", align_bytes=64)
-                pieces = [(half_width, H), (0, half_width)]
+                rooms = [(SIDE, grouped[:, SIDE:H, :]), (0, grouped[:, 0:SIDE, :])]
                 if e < LAST:
-                    split = (0, 0, half_width)[s] if e == 0 else VECTOR_COLUMNS
+                    split = (0, 0, SIDE)[s] if e == 0 else VECTOR_COLUMNS
                     if split > 0:
-                        round_columns(e, s, grouped, 0, split, nc.vector.tensor_copy)
-                    round_columns(e, s, grouped, split, H, nc.scalar.copy)
+                        round_columns(raw[(e, s)], grouped, 0, split, nc.vector.tensor_copy)
+                    round_columns(raw[(e, s)], grouped, split, H, nc.scalar.copy)
                 elif s < PASSES - 1:
-                    lower, upper = raw[(e, s)][:, :, 0:half_width], raw[(e, s)][:, :, half_width:H]
-                    round_side(lower, grouped, 0, None, 0, LG[s], nc.vector.tensor_copy)
-                    round_side(upper, grouped, 1, None, 0, P // 2, nc.scalar.copy)
-                    if LG[s] < P // 2:
-                        round_side(lower, grouped, 0, None, LG[s], P // 2, nc.scalar.copy)
-                else:
-                    round_side(raw_sides[0][:], grouped, 0, None, 0, SIDE_GROUPS[0], nc.vector.tensor_copy)
-                    round_side(raw_sides[0][:], grouped, 0, None, SIDE_GROUPS[0], P // 2, nc.scalar.copy)
-                    spare = windows[0][:, T : T + 2 * C].bitcast(BF16).rearrange("p (c j) -> p c j", j=4)
-                    rooms = [grouped[:, 0 : 2 * P, :], spare, grouped[:, 3 * P : 4 * P, :]]
+                    round_columns(raw[(e, s)], grouped, 0, VECTOR_COLUMNS, nc.vector.tensor_copy)
                     for u in range(2):
-                        round_side(raw_sides[1][:], rooms[1 + u], 1, u, 0, SIDE_GROUPS[1 + u], nc.vector.tensor_copy)
-                        round_side(raw_sides[1][:], rooms[1 + u], 1, u, SIDE_GROUPS[1 + u], P // 2, nc.scalar.copy)
-                    pieces = last_pieces
-                if pieces != last_pieces:
-                    rooms = [grouped[:, c0:c1, :] for c0, c1 in pieces]
-                for (c0, c1), room in zip(pieces, rooms):
-                    quantize(room, words, plane, c0, c1)
+                        c0, c1 = LAST_PIECES[1 + u]
+                        round_half(raw[(e, s)][:, :, SIDE:H], u, grouped[:, c0:c1, :], 0, SIDE // 4, nc.scalar.copy)
+                    round_columns(raw[(e, s)], grouped, VECTOR_COLUMNS, SIDE, nc.scalar.copy)
+                else:
+                    round_columns(raw_sides[0], grouped, 0, 4 * VECTOR_SIDE_GROUPS, nc.vector.tensor_copy)
+                    round_columns(raw_sides[0], grouped, 4 * VECTOR_SIDE_GROUPS, SIDE, nc.scalar.copy)
+                    rooms = [(0, grouped[:, 0:SIDE, :]), (SIDE, half_0_room), (SIDE + C, grouped[:, SIDE + C : H, :])]
+                    for u in range(2):
+                        room = rooms[1 + u][1]
+                        round_half(raw_sides[1][:], u, room, 0, VECTOR_SIDE_GROUPS, nc.vector.tensor_copy)
+                        round_half(raw_sides[1][:], u, room, VECTOR_SIDE_GROUPS, SIDE // 4, nc.scalar.copy)
+                for c0, room in rooms:
+                    c1 = c0 + room.shape[1]
+                    nc.vector.quantize_mx(
+                        out=words[:, c0:c1].bitcast(FP8X4),
+                        scales=plane[:, c0:c1],
+                        in_=room.rearrange("p c j -> p (c j)"),
+                    )
                 if e < LAST:
                     first_product(e, s, words, plane, 0, H, sums[e][:])
                 else:
-                    for (c0, c1), bank in zip(last_pieces, last_sums):
+                    for (c0, c1), bank in zip(LAST_PIECES, last_sums):
                         first_product(e, s, words, plane, c0, c1, bank[:])
                 if e > 0 and s == 0:
+                    c0 = 0 if e < LAST else H - C
+                    scaled = raw[(e, s)][:, :, c0 : c0 + C]
+                    sum_rows = sums[e - 1][:].rearrange("p (r c) -> p r c", c=C)
                     turned = psum.tile([P, 2 * C], F32, name="turned")
                     gated = ring.tile([P, H], BF16, name="gated", bufs=2)
-                    gate_product(
-                        e - 1,
-                        sums[e - 1][:].rearrange("p (r c) -> p r c", c=C),
-                        raw[(e, s)][:, :, 0:C] if e < LAST else raw[(e, s)][:, :, H - C : H],
-                        gated[:].rearrange("p (r c) -> p r c", c=C),
-                    )
+                    scale_by_gate(e - 1, sum_rows, scaled)
+                    gate_product(sum_rows, scaled, gated[:].rearrange("p (r c) -> p r c", c=C))
                     for u in range(2):
-                        nc.tensor.transpose(turned[:, P * u : P * (u + 1)], gated[:].bitcast(F32)[:, u : 2 * P : 2], identity[:])
+                        pair_words = gated[:].bitcast(F32)[:, u : 2 * P : 2]
+                        nc.tensor.transpose(turned[:, P * u : P * (u + 1)], pair_words, identity[:])
                 if 0 < e < LAST and s > 0:
-                    scatter(e - 1, s - 1, turned[:, C * (s - 1) : C * s], raw[(e, s)][:, 0, 0:C])
+                    pairs = raw[(e, s)][:, 0, 0:C]
+                    nc.scalar.copy(pairs, turned[:, C * (s - 1) : C * s])
+                    scatter(e - 1, s - 1, pairs)
 
         early_pairs = keep.tile([P, 2 * C], F32, name="early_pairs")
         nc.scalar.copy(early_pairs[:], turned[:])
-        entries = offsets[:, C * (LAST - 1) // 16 : C * LAST // 16]
-        nc.vector.tensor_copy(windows[0][:].indirect(entries), early_pairs[:, 0:C])
+        scatter(LAST - 1, 0, early_pairs[:, 0:C])
+
         last_gated = keep.tile([P, 2, 2, C], BF16, name="last_gated")
-        last_scaled = keep.tile([P, 3, C], F32, name="last_scaled")
+        side_0_scaled = keep.tile([P, SIDE], F32, name="side_0_scaled")
+        half_1_scaled = keep.tile([P, C], F32, name="half_1_scaled")
         last_pairs = keep.tile([P, 2, C], F32, name="last_pairs")
         last_turned = [psum.tile([P, C], F32, name="sums"), psum.tile([P, C], F32, name="last_turned", bufs=1)]
-        gate_product(
-            LAST, last_sums[0][:].rearrange("p (u c) -> p u c", u=2), last_scaled[:, 0:2, :], last_gated[:, :, 0, :]
-        )
-        gate_product(LAST, last_sums[1][:], windows[1][:, T : T + C], last_gated[:, 0, 1, :])
-        gate_product(LAST, last_sums[2][:], last_scaled[:, 2, :], last_gated[:, 1, 1, :])
+        scale_by_gate(LAST, last_sums[0][:], side_0_scaled[:])
+        for u in range(2):
+            gate_product(
+                last_sums[0][:].rearrange("p (m u d) -> p u m d", u=2, d=2)[:, u],
+                side_0_scaled[:].rearrange("p (m u d) -> p u m d", u=2, d=2)[:, u],
+                last_gated[:, u, 0, :].rearrange("p (m d) -> p m d", d=2),
+            )
+        for u, scaled in enumerate((half_0_scaled, half_1_scaled[:])):
+            scale_by_gate(LAST, last_sums[1 + u][:], scaled)
+            gate_product(last_sums[1 + u][:], scaled, last_gated[:, u, 1, :])
         for u in range(2):
             pair_words = last_gated[:, u].rearrange("p s c -> p (s c)").bitcast(F32)
             nc.tensor.transpose(last_turned[u][:], pair_words, identity[:])
-        nc.vector.tensor_copy(windows[1][:].indirect(entries), early_pairs[:, C : 2 * C])
+        scatter(LAST - 1, 1, early_pairs[:, C : 2 * C])
         for u in range(2):
-            scatter(LAST, u, last_turned[u][:], last_pairs[:, u, :])
+            nc.scalar.copy(last_pairs[:, u, :], last_turned[u][:])
+            scatter(LAST, u, last_pairs[:, u, :])
 
         both = keep.tile([P, 2, T], F32, name="both")
         nc.scalar.copy(both[:, 0, :], windows[0][:, 0:T])
@@ -218,7 +221,7 @@ def tile_moe_sdn_lin_relu2_kernel(
             interleave = nc.vector.tensor_copy if a < T // 2 else nc.scalar.copy
             interleave(c_in[a][:], both[:, :, a:b].rearrange("p u n -> p n u"))
 
-        bank_tags = [("last_sums_%d" % c0, 1) for c0, c1 in last_pieces] + [("last_turned", 1)]
+        bank_tags = [("last_sums_%d" % c0, 1) for c0, c1 in LAST_PIECES] + [("last_turned", 1)]
         bank_tags = bank_tags + [("sums", 2)] * 2 + [("turned", 2)] * 2
         banks = {}
         for a, b in TOKEN_CHUNKS:

@@ -24,6 +24,7 @@ GATHER = T // 2
 VECTOR_COLUMNS = 200
 VECTOR_SIDE_GROUPS = 42
 LAST_PIECES = [(0, SIDE), (SIDE, SIDE + C), (SIDE + C, H)]
+WARM_UP_PASSES = 4
 TOKEN_CHUNKS = [(0, 128), (128, 384), (384, 640), (640, 768)]
 
 
@@ -191,7 +192,7 @@ def tile_moe_sdn_lin_relu2_kernel(
         side_0_scaled = keep.tile([P, SIDE], F32, name="side_0_scaled")
         half_1_scaled = keep.tile([P, C], F32, name="half_1_scaled")
         last_pairs = keep.tile([P, 2, C], F32, name="last_pairs")
-        last_turned = [psum.tile([P, C], F32, name="sums"), psum.tile([P, C], F32, name="last_turned", bufs=1)]
+        last_turned = [psum.tile([P, C], F32, name="sums"), psum.tile([P, H], F32, name="last_turned", bufs=1)]
         scale_by_gate(LAST, last_sums[0][:], side_0_scaled[:])
         for u in range(2):
             gate_product(
@@ -204,11 +205,22 @@ def tile_moe_sdn_lin_relu2_kernel(
             gate_product(last_sums[1 + u][:], scaled, last_gated[:, u, 1, :])
         for u in range(2):
             pair_words = last_gated[:, u].rearrange("p s c -> p (s c)").bitcast(F32)
-            nc.tensor.transpose(last_turned[u][:], pair_words, identity[:])
+            nc.tensor.transpose(last_turned[u][:, 0:C], pair_words, identity[:])
         scatter(LAST - 1, 1, early_pairs[:, C : 2 * C])
         for u in range(2):
-            nc.scalar.copy(last_pairs[:, u, :], last_turned[u][:])
+            nc.scalar.copy(last_pairs[:, u, :], last_turned[u][:, 0:C])
             scatter(LAST, u, last_pairs[:, u, :])
+
+        for repeat in range(WARM_UP_PASSES):
+            nc.tensor.matmul_mx(
+                out=last_turned[1][:],
+                lhsT=slot_words[:, 0, 0:C].bitcast(FP8X4),
+                lhsT_scale=slot_plane[:, 0:C],
+                rhs=words[:].bitcast(FP8X4),
+                rhs_scale=plane[:],
+                start=True,
+                stop=True,
+            )
 
         both = keep.tile([P, 2, T], F32, name="both")
         nc.scalar.copy(both[:, 0, :], windows[0][:, 0:T])

@@ -257,8 +257,12 @@ def tile_moe_sdn_lin_relu2_kernel(
                     stop=True,
                 )
         for a, b in TOKEN_CHUNKS:
+            result = keep.tile([P, 2, b - a], F32, name="result_%d" % a)
+            rows = out[:, a:b].rearrange("(h p) n -> p h n", p=P)
             for h in range(2):
-                result = keep.tile([P, b - a], F32, name="result_%d_%d" % (a, h))
                 empty = nc.vector.tensor_copy if a > 0 and h == 0 else nc.scalar.copy
-                empty(result[:], banks[(a, h)][:])
-                nc.sync.dma_start(out[P * h : P * (h + 1), a:b], result[:])
+                empty(result[:, h, :], banks[(a, h)][:])
+                if (a, b) == TOKEN_CHUNKS[1]:
+                    nc.sync.dma_start(rows[:, h, :], result[:, h, :])
+            if (a, b) != TOKEN_CHUNKS[1]:
+                nc.sync.dma_start(rows, result[:])

@@ -22,10 +22,12 @@ LAST = E - 1
 SIDE = H // 2
 GATHER = T // 2
 VECTOR_COLUMNS = 200
-VECTOR_SIDE_GROUPS = 42
-LAST_PIECES = [(0, SIDE), (SIDE, SIDE + C), (SIDE + C, H)]
+VECTOR_LAST_GROUPS = 84
+VECTOR_GROUPS = 100
+LAST_PIECES = [(c0, c0 + C) for c0 in range(0, H, C)]
 WARM_UP_PASSES = 4
 TOKEN_CHUNKS = [(0, 128), (128, 384), (384, 640), (640, 768)]
+STORE_RANGES = [(0, 128), (128, 384), (384, 768)]
 
 
 def tile_moe_sdn_lin_relu2_kernel(
@@ -54,16 +56,11 @@ def tile_moe_sdn_lin_relu2_kernel(
         nc.sync.dma_start(x_tile[:, 0, :], x_words[0].rearrange("p t d -> p (t d)").bitcast(I32))
         nc.sync.dma_start(x_tile[:, 1:PASSES, :], x_words[1:PASSES].rearrange("s p t d -> p s (t d)").bitcast(I32))
         raw = {}
-        raw_sides = [keep.tile([P, 4, SIDE], F32, name="raw_side_%d" % side) for side in range(2)]
         for e in range(E):
             for s in range(PASSES):
                 rows = w1[e, 512 * s : 512 * (s + 1), :].rearrange("(p j) c -> p j c", j=4)
-                if (e, s) == (LAST, PASSES - 1):
-                    for side in range(2):
-                        nc.sync.dma_start(raw_sides[side][:], rows[:, :, SIDE * side : SIDE * (side + 1)])
-                else:
-                    raw[(e, s)] = keep.tile([P, 4, H], F32, name="raw_%d_%d" % (e, s))
-                    nc.sync.dma_start(raw[(e, s)][:], rows)
+                raw[(e, s)] = keep.tile([P, 4, H], F32, name="raw_%d_%d" % (e, s))
+                nc.sync.dma_start(raw[(e, s)][:], rows)
                 if (e, s) == (0, 0):
                     for q in range(4):
                         nc.sync.dma_start(
@@ -96,10 +93,10 @@ def tile_moe_sdn_lin_relu2_kernel(
                 source[:, :, c0:c1].rearrange("p j (c i) -> p c j i", i=4),
             )
 
-        def round_half(side, u, room, m0, m1, copy):
+        def round_half(source, u, room, m0, m1, copy):
             copy(
-                room.rearrange("p (m d) j -> p m j d", d=2)[:, m0:m1],
-                side.rearrange("p j (m u d) -> p u m j d", u=2, d=2)[:, u, m0:m1],
+                room.rearrange("p (m d) j -> p m j d", d=2),
+                source.rearrange("p j (m u d) -> p u m j d", u=2, d=2)[:, u, m0:m1],
             )
 
         def first_product(e, s, words, plane, c0, c1, sums):
@@ -121,8 +118,8 @@ def tile_moe_sdn_lin_relu2_kernel(
             nc.vector.scalar_tensor_tensor(gated, sums, 0.0, scaled, ALU.max, ALU.mult)
 
         windows = [keep.tile([P, T + C * (2 - u)], F32, name="window_%d" % u, align_bytes=64) for u in range(2)]
-        half_0_room = windows[0][:, T : T + 2 * C].bitcast(BF16).rearrange("p (c j) -> p c j", j=4)
-        half_0_scaled = windows[1][:, T : T + C]
+        piece_2_room = windows[0][:, T : T + 2 * C].bitcast(BF16).rearrange("p (c j) -> p c j", j=4)
+        piece_2_scaled = windows[1][:, T : T + C]
 
         def scatter(e, u, pairs):
             nc.vector.tensor_copy(windows[u][:].indirect(offsets[:, C * e // 16 : C * (e + 1) // 16]), pairs)
@@ -143,19 +140,18 @@ def tile_moe_sdn_lin_relu2_kernel(
                         round_columns(raw[(e, s)], grouped, 0, split, nc.vector.tensor_copy)
                     round_columns(raw[(e, s)], grouped, split, H, nc.scalar.copy)
                 elif s < PASSES - 1:
-                    round_columns(raw[(e, s)], grouped, 0, VECTOR_COLUMNS, nc.vector.tensor_copy)
-                    for u in range(2):
-                        c0, c1 = LAST_PIECES[1 + u]
-                        round_half(raw[(e, s)][:, :, SIDE:H], u, grouped[:, c0:c1, :], 0, SIDE // 4, nc.scalar.copy)
-                    round_columns(raw[(e, s)], grouped, VECTOR_COLUMNS, SIDE, nc.scalar.copy)
+                    split = 2 * VECTOR_GROUPS
+                    round_half(raw[(e, s)], 0, grouped[:, 0:split, :], 0, VECTOR_GROUPS, nc.vector.tensor_copy)
+                    round_half(raw[(e, s)], 1, grouped[:, SIDE:H, :], 0, P, nc.scalar.copy)
+                    round_half(raw[(e, s)], 0, grouped[:, split:SIDE, :], VECTOR_GROUPS, P, nc.scalar.copy)
                 else:
-                    round_columns(raw_sides[0], grouped, 0, 4 * VECTOR_SIDE_GROUPS, nc.vector.tensor_copy)
-                    round_columns(raw_sides[0], grouped, 4 * VECTOR_SIDE_GROUPS, SIDE, nc.scalar.copy)
-                    rooms = [(0, grouped[:, 0:SIDE, :]), (SIDE, half_0_room), (SIDE + C, grouped[:, SIDE + C : H, :])]
-                    for u in range(2):
-                        room = rooms[1 + u][1]
-                        round_half(raw_sides[1][:], u, room, 0, VECTOR_SIDE_GROUPS, nc.vector.tensor_copy)
-                        round_half(raw_sides[1][:], u, room, VECTOR_SIDE_GROUPS, SIDE // 4, nc.scalar.copy)
+                    split = 2 * VECTOR_LAST_GROUPS
+                    rooms = [(c0, piece_2_room if c0 == SIDE else grouped[:, c0:c1, :]) for c0, c1 in LAST_PIECES]
+                    round_half(raw[(e, s)], 0, grouped[:, 0:split, :], 0, VECTOR_LAST_GROUPS, nc.vector.tensor_copy)
+                    round_half(raw[(e, s)], 0, grouped[:, split:SIDE, :], VECTOR_LAST_GROUPS, P, nc.scalar.copy)
+                    round_half(raw[(e, s)], 1, piece_2_room, 0, P // 2, nc.vector.tensor_copy)
+                    round_half(raw[(e, s)], 1, grouped[:, SIDE + C : SIDE + split, :], P // 2, VECTOR_LAST_GROUPS, nc.vector.tensor_copy)
+                    round_half(raw[(e, s)], 1, grouped[:, SIDE + split : H, :], VECTOR_LAST_GROUPS, P, nc.scalar.copy)
                 for c0, room in rooms:
                     c1 = c0 + room.shape[1]
                     nc.vector.quantize_mx(
@@ -169,8 +165,7 @@ def tile_moe_sdn_lin_relu2_kernel(
                     for (c0, c1), bank in zip(LAST_PIECES, last_sums):
                         first_product(e, s, words, plane, c0, c1, bank[:])
                 if e > 0 and s == 0:
-                    c0 = 0 if e < LAST else H - C
-                    scaled = raw[(e, s)][:, :, c0 : c0 + C]
+                    scaled = raw[(e, s)][:, :, 0:C]
                     sum_rows = sums[e - 1][:].rearrange("p (r c) -> p r c", c=C)
                     turned = psum.tile([P, 2 * C], F32, name="turned")
                     gated = ring.tile([P, H], BF16, name="gated", bufs=2)
@@ -189,20 +184,13 @@ def tile_moe_sdn_lin_relu2_kernel(
         scatter(LAST - 1, 0, early_pairs[:, 0:C])
 
         last_gated = keep.tile([P, 2, 2, C], BF16, name="last_gated")
-        side_0_scaled = keep.tile([P, SIDE], F32, name="side_0_scaled")
-        half_1_scaled = keep.tile([P, C], F32, name="half_1_scaled")
+        last_scaled = keep.tile([P, 4, C], F32, name="last_scaled")
         last_pairs = keep.tile([P, 2, C], F32, name="last_pairs")
-        last_turned = [psum.tile([P, C], F32, name="sums"), psum.tile([P, H], F32, name="last_turned", bufs=1)]
-        scale_by_gate(LAST, last_sums[0][:], side_0_scaled[:])
-        for u in range(2):
-            gate_product(
-                last_sums[0][:].rearrange("p (m u d) -> p u m d", u=2, d=2)[:, u],
-                side_0_scaled[:].rearrange("p (m u d) -> p u m d", u=2, d=2)[:, u],
-                last_gated[:, u, 0, :].rearrange("p (m d) -> p m d", d=2),
-            )
-        for u, scaled in enumerate((half_0_scaled, half_1_scaled[:])):
-            scale_by_gate(LAST, last_sums[1 + u][:], scaled)
-            gate_product(last_sums[1 + u][:], scaled, last_gated[:, u, 1, :])
+        last_turned = [psum.tile([P, H], F32, name="sums") for u in range(2)]
+        for piece, bank in enumerate(last_sums):
+            scaled = piece_2_scaled if piece == 2 else last_scaled[:, piece, :]
+            scale_by_gate(LAST, bank[:], scaled)
+            gate_product(bank[:], scaled, last_gated[:, piece // 2, piece % 2, :])
         for u in range(2):
             pair_words = last_gated[:, u].rearrange("p s c -> p (s c)").bitcast(F32)
             nc.tensor.transpose(last_turned[u][:, 0:C], pair_words, identity[:])
@@ -224,16 +212,16 @@ def tile_moe_sdn_lin_relu2_kernel(
 
         both = keep.tile([P, 2, T], F32, name="both")
         nc.scalar.copy(both[:, 0, :], windows[0][:, 0:T])
-        nc.scalar.copy(both[:, 1, T // 2 : T], windows[1][:, T // 2 : T])
-        for a, b in TOKEN_CHUNKS[:2]:
-            nc.vector.tensor_copy(both[:, 1, a:b], windows[1][:, a:b])
+        for a, b in TOKEN_CHUNKS:
+            bring = nc.vector.tensor_copy if a < T // 2 else nc.scalar.copy
+            bring(both[:, 1, a:b], windows[1][:, a:b])
         c_in = {}
         for a, b in TOKEN_CHUNKS:
             c_in[a] = keep.tile([P, b - a, 2], F32, name="c_in_%d" % a, align_bytes=64)
             interleave = nc.vector.tensor_copy if a < T // 2 else nc.scalar.copy
             interleave(c_in[a][:], both[:, :, a:b].rearrange("p u n -> p n u"))
 
-        bank_tags = [("last_sums_%d" % c0, 1) for c0, c1 in LAST_PIECES] + [("last_turned", 1)]
+        bank_tags = [("last_sums_%d" % c0, 1) for c0, c1 in LAST_PIECES]
         bank_tags = bank_tags + [("sums", 2)] * 2 + [("turned", 2)] * 2
         banks = {}
         for a, b in TOKEN_CHUNKS:
@@ -256,13 +244,11 @@ def tile_moe_sdn_lin_relu2_kernel(
                     start=True,
                     stop=True,
                 )
-        for a, b in TOKEN_CHUNKS:
-            result = keep.tile([P, 2, b - a], F32, name="result_%d" % a)
-            rows = out[:, a:b].rearrange("(h p) n -> p h n", p=P)
+        for first, last in STORE_RANGES:
             for h in range(2):
-                empty = nc.vector.tensor_copy if a > 0 and h == 0 else nc.scalar.copy
-                empty(result[:, h, :], banks[(a, h)][:])
-                if (a, b) == TOKEN_CHUNKS[1]:
-                    nc.sync.dma_start(rows[:, h, :], result[:, h, :])
-            if (a, b) != TOKEN_CHUNKS[1]:
-                nc.sync.dma_start(rows, result[:])
+                result = keep.tile([P, last - first], F32, name="result_%d_%d" % (first, h))
+                empty = nc.vector.tensor_copy if first > 0 and h == 1 else nc.scalar.copy
+                for a, b in TOKEN_CHUNKS:
+                    if first <= a < last:
+                        empty(result[:, a - first : b - first], banks[(a, h)][:])
+                nc.sync.dma_start(out[P * h : P * (h + 1), first:last], result[:])

@@ -53,8 +53,9 @@ def tile_moe_sdn_lin_relu2_kernel(
 
         x_tile = keep.tile([P, PASSES, T], I32, name="x_tile", align_bytes=64)
         w2_tile = keep.tile([P, N], I32, name="w2_tile", align_bytes=64)
-        nc.sync.dma_start(x_tile[:, 0, :], x_words[0].rearrange("p t d -> p (t d)").bitcast(I32))
-        nc.sync.dma_start(x_tile[:, 1:PASSES, :], x_words[1:PASSES].rearrange("s p t d -> p s (t d)").bitcast(I32))
+        for s in range(PASSES):
+            queue = nc.sync if s == 1 else nc.scalar
+            queue.dma_start(x_tile[:, s, :], x_words[s].rearrange("p t d -> p (t d)").bitcast(I32))
         raw = {}
         for e in range(E):
             for s in range(PASSES):

@@ -26,6 +26,7 @@ VECTOR_LAST_GROUPS = 84
 VECTOR_GROUPS = 100
 LAST_PIECES = [(c0, c0 + C) for c0 in range(0, H, C)]
 WARM_UP_PASSES = 4
+DMA_ALIGN = 256
 TOKEN_CHUNKS = [(0, 128), (128, 384), (384, 640), (640, 768)]
 STORE_RANGES = [(0, 128), (128, 384), (384, 768)]
 
@@ -42,7 +43,7 @@ def tile_moe_sdn_lin_relu2_kernel(
         offsets = keep.tile([P, T // 16], U16, name="offsets")
         nc.sync.dma_start(offsets[:], offs)
 
-        x_plane = keep.tile([P, T // 4], I32, name="x_plane", align_bytes=64)
+        x_plane = keep.tile([P, T // 4], I32, name="x_plane", align_bytes=DMA_ALIGN)
         w2_plane = keep.tile([P, N // 4], I32, name="w2_plane", align_bytes=64)
         gate_rows = keep.tile([P, C], F32, name="gate_rows")
         identity = keep.tile([P, P], F32, name="identity")
@@ -51,8 +52,8 @@ def tile_moe_sdn_lin_relu2_kernel(
         nc.vector.memset(gate_rows[:], 0.0)
         make_identity(nc, identity[:])
 
-        x_tile = keep.tile([P, PASSES, T], I32, name="x_tile", align_bytes=64)
-        w2_tile = keep.tile([P, N], I32, name="w2_tile", align_bytes=64)
+        x_tile = keep.tile([P, PASSES, T], I32, name="x_tile", align_bytes=DMA_ALIGN)
+        w2_tile = keep.tile([P, N], I32, name="w2_tile", align_bytes=DMA_ALIGN)
         for s in range(PASSES):
             queue = nc.sync if s == 1 else nc.scalar
             queue.dma_start(x_tile[:, s, :], x_words[s].rearrange("p t d -> p (t d)").bitcast(I32))
@@ -60,7 +61,7 @@ def tile_moe_sdn_lin_relu2_kernel(
         for e in range(E):
             for s in range(PASSES):
                 rows = w1[e, 512 * s : 512 * (s + 1), :].rearrange("(p j) c -> p j c", j=4)
-                raw[(e, s)] = keep.tile([P, 4, H], F32, name="raw_%d_%d" % (e, s))
+                raw[(e, s)] = keep.tile([P, 4, H], F32, name="raw_%d_%d" % (e, s), align_bytes=DMA_ALIGN)
                 nc.sync.dma_start(raw[(e, s)][:], rows)
                 if (e, s) == (0, 0):
                     for q in range(4):
@@ -247,7 +248,7 @@ def tile_moe_sdn_lin_relu2_kernel(
                 )
         for first, last in STORE_RANGES:
             for h in range(2):
-                result = keep.tile([P, last - first], F32, name="result_%d_%d" % (first, h))
+                result = keep.tile([P, last - first], F32, name="result_%d_%d" % (first, h), align_bytes=DMA_ALIGN)
                 empty = nc.vector.tensor_copy if first > 0 and h == 1 else nc.scalar.copy
                 for a, b in TOKEN_CHUNKS:
                     if first <= a < last:

@@ -22,9 +22,10 @@ LAST = E - 1
 SIDE = H // 2
 GATHER = T // 2
 VECTOR_COLUMNS = 200
-VECTOR_LAST_GROUPS = 84
-VECTOR_GROUPS = 100
-LAST_PIECES = [(c0, c0 + C) for c0 in range(0, H, C)]
+VECTOR_SIDE_GROUPS = 42
+HELD_ROOM = 0
+HELD_SCALED = 1
+LAST_PIECES = [(0, SIDE), (SIDE, SIDE + C), (SIDE + C, H)]
 WARM_UP_PASSES = 4
 DMA_ALIGN = 256
 TOKEN_CHUNKS = [(0, 128), (128, 384), (384, 640), (640, 768)]
@@ -61,6 +62,11 @@ def tile_moe_sdn_lin_relu2_kernel(
         for e in range(E):
             for s in range(PASSES):
                 rows = w1[e, 512 * s : 512 * (s + 1), :].rearrange("(p j) c -> p j c", j=4)
+                if (e, s) == (LAST, PASSES - 1):
+                    sides = [keep.tile([P, 4, SIDE], F32, name="side_%d" % v, align_bytes=DMA_ALIGN) for v in range(2)]
+                    for v in range(2):
+                        nc.sync.dma_start(sides[v][:], rows[:, :, SIDE * v : SIDE * (v + 1)])
+                    continue
                 raw[(e, s)] = keep.tile([P, 4, H], F32, name="raw_%d_%d" % (e, s), align_bytes=DMA_ALIGN)
                 nc.sync.dma_start(raw[(e, s)][:], rows)
                 if (e, s) == (0, 0):
@@ -120,8 +126,8 @@ def tile_moe_sdn_lin_relu2_kernel(
             nc.vector.scalar_tensor_tensor(gated, sums, 0.0, scaled, ALU.max, ALU.mult)
 
         windows = [keep.tile([P, T + C * (2 - u)], F32, name="window_%d" % u, align_bytes=64) for u in range(2)]
-        piece_2_room = windows[0][:, T : T + 2 * C].bitcast(BF16).rearrange("p (c j) -> p c j", j=4)
-        piece_2_scaled = windows[1][:, T : T + C]
+        held_room = windows[0][:, T : T + 2 * C].bitcast(BF16).rearrange("p (c j) -> p c j", j=4)
+        held_scaled = windows[1][:, T : T + C]
 
         def scatter(e, u, pairs):
             nc.vector.tensor_copy(windows[u][:].indirect(offsets[:, C * e // 16 : C * (e + 1) // 16]), pairs)
@@ -142,18 +148,23 @@ def tile_moe_sdn_lin_relu2_kernel(
                         round_columns(raw[(e, s)], grouped, 0, split, nc.vector.tensor_copy)
                     round_columns(raw[(e, s)], grouped, split, H, nc.scalar.copy)
                 elif s < PASSES - 1:
-                    split = 2 * VECTOR_GROUPS
-                    round_half(raw[(e, s)], 0, grouped[:, 0:split, :], 0, VECTOR_GROUPS, nc.vector.tensor_copy)
-                    round_half(raw[(e, s)], 1, grouped[:, SIDE:H, :], 0, P, nc.scalar.copy)
-                    round_half(raw[(e, s)], 0, grouped[:, split:SIDE, :], VECTOR_GROUPS, P, nc.scalar.copy)
+                    round_columns(raw[(e, s)], grouped, 0, VECTOR_COLUMNS, nc.vector.tensor_copy)
+                    nc.scalar.copy(
+                        grouped[:, SIDE:H, :].rearrange("p (u m d) j -> p m u j d", u=2, d=2),
+                        raw[(e, s)][:, :, SIDE:H].rearrange("p j (m u d) -> p m u j d", u=2, d=2),
+                    )
+                    round_columns(raw[(e, s)], grouped, VECTOR_COLUMNS, SIDE, nc.scalar.copy)
                 else:
-                    split = 2 * VECTOR_LAST_GROUPS
-                    rooms = [(c0, piece_2_room if c0 == SIDE else grouped[:, c0:c1, :]) for c0, c1 in LAST_PIECES]
-                    round_half(raw[(e, s)], 0, grouped[:, 0:split, :], 0, VECTOR_LAST_GROUPS, nc.vector.tensor_copy)
-                    round_half(raw[(e, s)], 0, grouped[:, split:SIDE, :], VECTOR_LAST_GROUPS, P, nc.scalar.copy)
-                    round_half(raw[(e, s)], 1, piece_2_room, 0, P // 2, nc.vector.tensor_copy)
-                    round_half(raw[(e, s)], 1, grouped[:, SIDE + C : SIDE + split, :], P // 2, VECTOR_LAST_GROUPS, nc.vector.tensor_copy)
-                    round_half(raw[(e, s)], 1, grouped[:, SIDE + split : H, :], VECTOR_LAST_GROUPS, P, nc.scalar.copy)
+                    groups = VECTOR_SIDE_GROUPS
+                    round_columns(sides[0], grouped, 0, 4 * groups, nc.vector.tensor_copy)
+                    round_columns(sides[0], grouped, 4 * groups, SIDE, nc.scalar.copy)
+                    rooms = [(0, grouped[:, 0:SIDE, :])]
+                    for u in range(2):
+                        c0 = SIDE + C * u
+                        room = held_room if u == HELD_ROOM else grouped[:, c0 : c0 + C, :]
+                        round_half(sides[1], u, room[:, 0 : 2 * groups, :], 0, groups, nc.vector.tensor_copy)
+                        round_half(sides[1], u, room[:, 2 * groups : C, :], groups, C // 2, nc.scalar.copy)
+                        rooms.append((c0, room))
                 for c0, room in rooms:
                     c1 = c0 + room.shape[1]
                     nc.vector.quantize_mx(
@@ -167,7 +178,7 @@ def tile_moe_sdn_lin_relu2_kernel(
                     for (c0, c1), bank in zip(LAST_PIECES, last_sums):
                         first_product(e, s, words, plane, c0, c1, bank[:])
                 if e > 0 and s == 0:
-                    scaled = raw[(e, s)][:, :, 0:C]
+                    scaled = raw[(e, s)][:, :, 0:C] if e < LAST else raw[(e, s)][:, :, H - C : H]
                     sum_rows = sums[e - 1][:].rearrange("p (r c) -> p r c", c=C)
                     turned = psum.tile([P, 2 * C], F32, name="turned")
                     gated = ring.tile([P, H], BF16, name="gated", bufs=2)
@@ -186,13 +197,20 @@ def tile_moe_sdn_lin_relu2_kernel(
         scatter(LAST - 1, 0, early_pairs[:, 0:C])
 
         last_gated = keep.tile([P, 2, 2, C], BF16, name="last_gated")
-        last_scaled = keep.tile([P, 4, C], F32, name="last_scaled")
+        last_scaled = keep.tile([P, SIDE + C], F32, name="last_scaled")
         last_pairs = keep.tile([P, 2, C], F32, name="last_pairs")
         last_turned = [psum.tile([P, H], F32, name="sums") for u in range(2)]
-        for piece, bank in enumerate(last_sums):
-            scaled = piece_2_scaled if piece == 2 else last_scaled[:, piece, :]
-            scale_by_gate(LAST, bank[:], scaled)
-            gate_product(bank[:], scaled, last_gated[:, piece // 2, piece % 2, :])
+        scale_by_gate(LAST, last_sums[0][:], last_scaled[:, 0:SIDE])
+        for u in range(2):
+            gate_product(
+                last_sums[0][:].rearrange("p (m u d) -> p u m d", u=2, d=2)[:, u],
+                last_scaled[:, 0:SIDE].rearrange("p (m u d) -> p u m d", u=2, d=2)[:, u],
+                last_gated[:, u, 0, :].rearrange("p (m d) -> p m d", d=2),
+            )
+        for u in range(2):
+            scaled = held_scaled if u == HELD_SCALED else last_scaled[:, SIDE : SIDE + C]
+            scale_by_gate(LAST, last_sums[1 + u][:], scaled)
+            gate_product(last_sums[1 + u][:], scaled, last_gated[:, u, 1, :])
         for u in range(2):
             pair_words = last_gated[:, u].rearrange("p s c -> p (s c)").bitcast(F32)
             nc.tensor.transpose(last_turned[u][:, 0:C], pair_words, identity[:])
@@ -224,7 +242,7 @@ def tile_moe_sdn_lin_relu2_kernel(
             interleave(c_in[a][:], both[:, :, a:b].rearrange("p u n -> p n u"))
 
         bank_tags = [("last_sums_%d" % c0, 1) for c0, c1 in LAST_PIECES]
-        bank_tags = bank_tags + [("sums", 2)] * 2 + [("turned", 2)] * 2
+        bank_tags = bank_tags + [("spare", 1)] + [("sums", 2)] * 2 + [("turned", 2)] * 2
         banks = {}
         for a, b in TOKEN_CHUNKS:
             c_words = keep.tile([P, b - a], U32, name="c_words_%d" % a, align_bytes=64)

@@ -26,7 +26,6 @@ VECTOR_SIDE_GROUPS = 42
 HELD_ROOM = 0
 HELD_SCALED = 1
 LAST_PIECES = [(0, SIDE), (SIDE, SIDE + C), (SIDE + C, H)]
-WARM_UP_PASSES = 4
 DMA_ALIGN = 256
 TOKEN_CHUNKS = [(0, 128), (128, 384), (384, 640), (640, 768)]
 STORE_RANGES = [(0, 128), (128, 384), (384, 768)]
@@ -218,17 +217,6 @@ def tile_moe_sdn_lin_relu2_kernel(
         for u in range(2):
             nc.scalar.copy(last_pairs[:, u, :], last_turned[u][:, 0:C])
             scatter(LAST, u, last_pairs[:, u, :])
-
-        for repeat in range(WARM_UP_PASSES):
-            nc.tensor.matmul_mx(
-                out=last_turned[1][:],
-                lhsT=slot_words[:, 0, 0:C].bitcast(FP8X4),
-                lhsT_scale=slot_plane[:, 0:C],
-                rhs=words[:].bitcast(FP8X4),
-                rhs_scale=plane[:],
-                start=True,
-                stop=True,
-            )
 
         both = keep.tile([P, 2, T], F32, name="both")
         nc.scalar.copy(both[:, 0, :], windows[0][:, 0:T])

@@ -26,6 +26,7 @@ VECTOR_SIDE_GROUPS = 42
 HELD_ROOM = 0
 HELD_SCALED = 1
 LAST_PIECES = [(0, SIDE), (SIDE, SIDE + C), (SIDE + C, H)]
+WARM_UP_PASSES = 2
 DMA_ALIGN = 256
 TOKEN_CHUNKS = [(0, 128), (128, 384), (384, 640), (640, 768)]
 STORE_RANGES = [(0, 128), (128, 384), (384, 768)]
@@ -217,6 +218,17 @@ def tile_moe_sdn_lin_relu2_kernel(
         for u in range(2):
             nc.scalar.copy(last_pairs[:, u, :], last_turned[u][:, 0:C])
             scatter(LAST, u, last_pairs[:, u, :])
+
+        for repeat in range(WARM_UP_PASSES):
+            nc.tensor.matmul_mx(
+                out=last_turned[1][:],
+                lhsT=slot_words[:, 0, 0:C].bitcast(FP8X4),
+                lhsT_scale=slot_plane[:, 0:C],
+                rhs=words[:].bitcast(FP8X4),
+                rhs_scale=plane[:],
+                start=True,
+                stop=True,
+            )
 
         both = keep.tile([P, 2, T], F32, name="both")
         nc.scalar.copy(both[:, 0, :], windows[0][:, 0:T])

@@ -54,7 +54,6 @@ def tile_moe_sdn_lin_relu2_kernel(
         make_identity(nc, identity[:])
 
         x_tile = keep.tile([P, PASSES, T], I32, name="x_tile", align_bytes=DMA_ALIGN)
-        w2_tile = keep.tile([P, N], I32, name="w2_tile", align_bytes=DMA_ALIGN)
         for s in range(PASSES):
             queue = nc.sync if s == 1 else nc.scalar
             queue.dma_start(x_tile[:, s, :], x_words[s].rearrange("p t d -> p (t d)").bitcast(I32))
@@ -76,7 +75,6 @@ def tile_moe_sdn_lin_relu2_kernel(
                         )
                 if (e, s) == (0, PASSES - 1):
                     nc.sync.dma_start(gate_rows[0:E, :], gate[0].rearrange("(e c) -> e c", e=E))
-        nc.sync.dma_start(w2_tile[:], w2_words[0].rearrange("p n d -> p (n d)").bitcast(I32))
         for q in range(4):
             nc.sync.dma_start(w2_plane[32 * q : 32 * q + 4, :], w2_scales[0, 4 * q : 4 * q + 4, :].bitcast(I32))
 
@@ -197,7 +195,7 @@ def tile_moe_sdn_lin_relu2_kernel(
         scatter(LAST - 1, 0, early_pairs[:, 0:C])
 
         last_gated = keep.tile([P, 2, 2, C], BF16, name="last_gated")
-        last_scaled = keep.tile([P, SIDE + C], F32, name="last_scaled")
+        last_scaled = keep.tile([P, SIDE + C], F32, name="last_scaled", align_bytes=DMA_ALIGN)
         last_pairs = keep.tile([P, 2, C], F32, name="last_pairs")
         last_turned = [psum.tile([P, H], F32, name="sums") for u in range(2)]
         scale_by_gate(LAST, last_sums[0][:], last_scaled[:, 0:SIDE])
@@ -219,11 +217,14 @@ def tile_moe_sdn_lin_relu2_kernel(
             nc.scalar.copy(last_pairs[:, u, :], last_turned[u][:, 0:C])
             scatter(LAST, u, last_pairs[:, u, :])
 
+        w2_tile = keep.tile([P, N], I32, name="w2_tile", tag="last_scaled", align_bytes=DMA_ALIGN)
+        nc.sync.dma_start(w2_tile[:], w2_words[0].rearrange("p n d -> p (n d)").bitcast(I32))
+
         for repeat in range(WARM_UP_PASSES):
             nc.tensor.matmul_mx(
                 out=last_turned[1][:],
-                lhsT=slot_words[:, 0, 0:C].bitcast(FP8X4),
-                lhsT_scale=slot_plane[:, 0:C],
+                lhsT=w2_tile[:, 0:P].bitcast(FP8X4),
+                lhsT_scale=w2_plane[:].bitcast(U8)[:, 0:P],
                 rhs=words[:].bitcast(FP8X4),
                 rhs_scale=plane[:],
                 start=True,

@@ -24,7 +24,7 @@ GATHER = T // 2
 VECTOR_COLUMNS = 200
 VECTOR_SIDE_GROUPS = 42
 HELD_ROOM = 0
-HELD_SCALED = 1
+HELD_SCALED = 0
 LAST_PIECES = [(0, SIDE), (SIDE, SIDE + C), (SIDE + C, H)]
 WARM_UP_PASSES = 2
 DMA_ALIGN = 256

@@ -142,7 +142,16 @@ def tile_moe_sdn_lin_relu2_kernel(
                 rooms = [(SIDE, grouped[:, SIDE:H, :]), (0, grouped[:, 0:SIDE, :])]
                 if e < LAST:
                     split = (0, 0, SIDE)[s] if e == 0 else VECTOR_COLUMNS
-                    if split > 0:
+                    if e > 0:
+                        nc.gpsimd.tensor_scalar(
+                            grouped[:, 0:split, :],
+                            raw[(e, s)][:, :, 0:split].rearrange("p j c -> p c j"),
+                            1.0,
+                            0.0,
+                            ALU.mult,
+                            ALU.add,
+                        )
+                    elif split > 0:
                         round_columns(raw[(e, s)], grouped, 0, split, nc.vector.tensor_copy)
                     round_columns(raw[(e, s)], grouped, split, H, nc.scalar.copy)
                 elif s < PASSES - 1:

from contextlib import ExitStack

import concourse.mybir as mybir
from concourse.masks import make_identity

K, T, E, C, H, N = 1536, 768, 6, 128, 512, 256
FLOPS = 2 * K * H * E * C + 2 * H * N * T

F32 = mybir.dt.float32
BF16 = mybir.dt.bfloat16
I32 = mybir.dt.int32
U32 = mybir.dt.uint32
U16 = mybir.dt.uint16
U8 = mybir.dt.uint8
FP8X4 = mybir.dt.float8_e4m3fn_x4
ACT = mybir.ActivationFunctionType
ALU = mybir.AluOpType

P = 128
PASSES = K // 512
LAST = E - 1
SIDE = H // 2
GATHER = T // 2
VECTOR_COLUMNS = 200
VECTOR_SIDE_GROUPS = 42
HELD_ROOM = 0
HELD_SCALED = 0
LAST_PIECES = [(0, SIDE), (SIDE, SIDE + C), (SIDE + C, H)]
WARM_UP_PASSES = 2
DMA_ALIGN = 256
TOKEN_CHUNKS = [(0, 128), (128, 384), (384, 640), (640, 768)]
STORE_RANGES = [(0, 128), (128, 384), (384, 768)]


def tile_moe_sdn_lin_relu2_kernel(
    tc, x_words, x_scales, w1, w2_words, w2_scales, gate, offs, out
):
    nc = tc.nc
    with ExitStack() as ctx:
        keep = ctx.enter_context(tc.tile_pool(name="keep", bufs=1))
        ring = ctx.enter_context(tc.tile_pool(name="ring", bufs=4))
        psum = ctx.enter_context(tc.psum_pool(name="psum", bufs=2))

        offsets = keep.tile([P, T // 16], U16, name="offsets")
        nc.sync.dma_start(offsets[:], offs)

        x_plane = keep.tile([P, T // 4], I32, name="x_plane", align_bytes=DMA_ALIGN)
        w2_plane = keep.tile([P, N // 4], I32, name="w2_plane", align_bytes=64)
        gate_rows = keep.tile([P, C], F32, name="gate_rows")
        identity = keep.tile([P, P], F32, name="identity")
        nc.vector.memset(x_plane[:], 0)
        nc.vector.memset(w2_plane[:], 0)
        nc.vector.memset(gate_rows[:], 0.0)
        make_identity(nc, identity[:])

        x_tile = keep.tile([P, PASSES, T], I32, name="x_tile", align_bytes=DMA_ALIGN)
        for s in range(PASSES):
            queue = nc.sync if s == 1 else nc.scalar
            queue.dma_start(x_tile[:, s, :], x_words[s].rearrange("p t d -> p (t d)").bitcast(I32))
        raw = {}
        for e in range(E):
            for s in range(PASSES):
                rows = w1[e, 512 * s : 512 * (s + 1), :].rearrange("(p j) c -> p j c", j=4)
                if (e, s) == (LAST, PASSES - 1):
                    sides = [keep.tile([P, 4, SIDE], F32, name="side_%d" % v, align_bytes=DMA_ALIGN) for v in range(2)]
                    for v in range(2):
                        nc.sync.dma_start(sides[v][:], rows[:, :, SIDE * v : SIDE * (v + 1)])
                    continue
                raw[(e, s)] = keep.tile([P, 4, H], F32, name="raw_%d_%d" % (e, s), align_bytes=DMA_ALIGN)
                nc.sync.dma_start(raw[(e, s)][:], rows)
                if (e, s) == (0, 0):
                    for q in range(4):
                        nc.sync.dma_start(
                            x_plane[32 * q : 32 * q + 4 * PASSES, :], x_scales[:, 4 * q : 4 * q + 4, :].bitcast(I32)
                        )
                if (e, s) == (0, PASSES - 1):
                    nc.sync.dma_start(gate_rows[0:E, :], gate[0].rearrange("(e c) -> e c", e=E))
        for q in range(4):
            nc.sync.dma_start(w2_plane[32 * q : 32 * q + 4, :], w2_scales[0, 4 * q : 4 * q + 4, :].bitcast(I32))

        slot_words = keep.tile([P, PASSES, T], U32, name="slot_words", align_bytes=64)
        slot_plane = keep.tile([P, T], U8, name="slot_plane", align_bytes=64)
        for s in range(PASSES):
            for a in range(0, T, GATHER):
                entries = offsets[:, a // 16 : (a + GATHER) // 16]
                nc.vector.tensor_copy(slot_words[:, s, a : a + GATHER], x_tile[:, s, :].bitcast(U32).indirect(entries))
        for a in range(0, T, GATHER):
            entries = offsets[:, a // 16 : (a + GATHER) // 16]
            nc.vector.tensor_copy(slot_plane[:, a : a + GATHER], x_plane[:].bitcast(U8).indirect(entries))

        gate_bank = psum.tile([P, P], F32, name="turned")
        nc.tensor.transpose(gate_bank[:], gate_rows[:], identity[:])
        gate_columns = keep.tile([P, E], F32, name="gate_columns")
        nc.scalar.copy(gate_columns[:], gate_bank[:, 0:E])

        def round_columns(source, grouped, c0, c1, copy):
            copy(
                grouped[:, c0:c1, :].rearrange("p (c i) j -> p c j i", i=4),
                source[:, :, c0:c1].rearrange("p j (c i) -> p c j i", i=4),
            )

        def round_half(source, u, room, m0, m1, copy):
            copy(
                room.rearrange("p (m d) j -> p m j d", d=2),
                source.rearrange("p j (m u d) -> p u m j d", u=2, d=2)[:, u, m0:m1],
            )

        def first_product(e, s, words, plane, c0, c1, sums):
            slots = slice(C * e, C * (e + 1))
            nc.tensor.matmul_mx(
                out=sums,
                lhsT=slot_words[:, s, slots].bitcast(FP8X4),
                lhsT_scale=slot_plane[4 * s : P, slots],
                rhs=words[:, c0:c1].bitcast(FP8X4),
                rhs_scale=plane[:, c0:c1],
                start=(s == 0),
                stop=(s == PASSES - 1),
            )

        def scale_by_gate(e, sums, scaled):
            nc.scalar.activation(scaled, sums, ACT.Copy, scale=gate_columns[:, e : e + 1])

        def gate_product(sums, scaled, gated):
            nc.vector.scalar_tensor_tensor(gated, sums, 0.0, scaled, ALU.max, ALU.mult)

        windows = [keep.tile([P, T + C * (2 - u)], F32, name="window_%d" % u, align_bytes=64) for u in range(2)]
        held_room = windows[0][:, T : T + 2 * C].bitcast(BF16).rearrange("p (c j) -> p c j", j=4)
        held_scaled = windows[1][:, T : T + C]

        def scatter(e, u, pairs):
            nc.vector.tensor_copy(windows[u][:].indirect(offsets[:, C * e // 16 : C * (e + 1) // 16]), pairs)

        last_sums = [psum.tile([P, c1 - c0], F32, name="last_sums_%d" % c0, bufs=1) for c0, c1 in LAST_PIECES]
        sums = {}
        for e in range(E):
            if e < LAST:
                sums[e] = psum.tile([P, H], F32, name="sums")
            for s in range(PASSES):
                grouped = ring.tile([P, H, 4], BF16, name="grouped", align_bytes=64)
                words = ring.tile([P, H], U32, name="w1_words", align_bytes=64)
                plane = ring.tile([P, H], U8, name="w1_plane", align_bytes=64)
                rooms = [(SIDE, grouped[:, SIDE:H, :]), (0, grouped[:, 0:SIDE, :])]
                if e < LAST:
                    split = (0, 0, SIDE)[s] if e == 0 else VECTOR_COLUMNS
                    if e > 0:
                        nc.gpsimd.tensor_scalar(
                            grouped[:, 0:split, :],
                            raw[(e, s)][:, :, 0:split].rearrange("p j c -> p c j"),
                            1.0,
                            0.0,
                            ALU.mult,
                            ALU.add,
                        )
                    elif split > 0:
                        round_columns(raw[(e, s)], grouped, 0, split, nc.vector.tensor_copy)
                    round_columns(raw[(e, s)], grouped, split, H, nc.scalar.copy)
                elif s < PASSES - 1:
                    round_columns(raw[(e, s)], grouped, 0, VECTOR_COLUMNS, nc.vector.tensor_copy)
                    nc.scalar.copy(
                        grouped[:, SIDE:H, :].rearrange("p (u m d) j -> p m u j d", u=2, d=2),
                        raw[(e, s)][:, :, SIDE:H].rearrange("p j (m u d) -> p m u j d", u=2, d=2),
                    )
                    round_columns(raw[(e, s)], grouped, VECTOR_COLUMNS, SIDE, nc.scalar.copy)
                else:
                    groups = VECTOR_SIDE_GROUPS
                    round_columns(sides[0], grouped, 0, 4 * groups, nc.vector.tensor_copy)
                    round_columns(sides[0], grouped, 4 * groups, SIDE, nc.scalar.copy)
                    rooms = [(0, grouped[:, 0:SIDE, :])]
                    for u in range(2):
                        c0 = SIDE + C * u
                        room = held_room if u == HELD_ROOM else grouped[:, c0 : c0 + C, :]
                        round_half(sides[1], u, room[:, 0 : 2 * groups, :], 0, groups, nc.vector.tensor_copy)
                        round_half(sides[1], u, room[:, 2 * groups : C, :], groups, C // 2, nc.scalar.copy)
                        rooms.append((c0, room))
                for c0, room in rooms:
                    c1 = c0 + room.shape[1]
                    nc.vector.quantize_mx(
                        out=words[:, c0:c1].bitcast(FP8X4),
                        scales=plane[:, c0:c1],
                        in_=room.rearrange("p c j -> p (c j)"),
                    )
                if e < LAST:
                    first_product(e, s, words, plane, 0, H, sums[e][:])
                else:
                    for (c0, c1), bank in zip(LAST_PIECES, last_sums):
                        first_product(e, s, words, plane, c0, c1, bank[:])
                if e > 0 and s == 0:
                    scaled = raw[(e, s)][:, :, 0:C] if e < LAST else raw[(e, s)][:, :, H - C : H]
                    sum_rows = sums[e - 1][:].rearrange("p (r c) -> p r c", c=C)
                    turned = psum.tile([P, 2 * C], F32, name="turned")
                    gated = ring.tile([P, H], BF16, name="gated", bufs=2)
                    scale_by_gate(e - 1, sum_rows, scaled)
                    gate_product(sum_rows, scaled, gated[:].rearrange("p (r c) -> p r c", c=C))
                    for u in range(2):
                        pair_words = gated[:].bitcast(F32)[:, u : 2 * P : 2]
                        nc.tensor.transpose(turned[:, P * u : P * (u + 1)], pair_words, identity[:])
                if 0 < e < LAST and s > 0:
                    pairs = raw[(e, s)][:, 0, 0:C]
                    nc.scalar.copy(pairs, turned[:, C * (s - 1) : C * s])
                    scatter(e - 1, s - 1, pairs)

        early_pairs = keep.tile([P, 2 * C], F32, name="early_pairs")
        nc.scalar.copy(early_pairs[:], turned[:])
        scatter(LAST - 1, 0, early_pairs[:, 0:C])

        last_gated = keep.tile([P, 2, 2, C], BF16, name="last_gated")
        last_scaled = keep.tile([P, SIDE + C], F32, name="last_scaled", align_bytes=DMA_ALIGN)
        last_pairs = keep.tile([P, 2, C], F32, name="last_pairs")
        last_turned = [psum.tile([P, H], F32, name="sums") for u in range(2)]
        scale_by_gate(LAST, last_sums[0][:], last_scaled[:, 0:SIDE])
        for u in range(2):
            gate_product(
                last_sums[0][:].rearrange("p (m u d) -> p u m d", u=2, d=2)[:, u],
                last_scaled[:, 0:SIDE].rearrange("p (m u d) -> p u m d", u=2, d=2)[:, u],
                last_gated[:, u, 0, :].rearrange("p (m d) -> p m d", d=2),
            )
        for u in range(2):
            scaled = held_scaled if u == HELD_SCALED else last_scaled[:, SIDE : SIDE + C]
            scale_by_gate(LAST, last_sums[1 + u][:], scaled)
            gate_product(last_sums[1 + u][:], scaled, last_gated[:, u, 1, :])
        for u in range(2):
            pair_words = last_gated[:, u].rearrange("p s c -> p (s c)").bitcast(F32)
            nc.tensor.transpose(last_turned[u][:, 0:C], pair_words, identity[:])
        scatter(LAST - 1, 1, early_pairs[:, C : 2 * C])
        for u in range(2):
            nc.scalar.copy(last_pairs[:, u, :], last_turned[u][:, 0:C])
            scatter(LAST, u, last_pairs[:, u, :])

        w2_tile = keep.tile([P, N], I32, name="w2_tile", tag="last_scaled", align_bytes=DMA_ALIGN)
        nc.sync.dma_start(w2_tile[:], w2_words[0].rearrange("p n d -> p (n d)").bitcast(I32))

        for repeat in range(WARM_UP_PASSES):
            nc.tensor.matmul_mx(
                out=last_turned[1][:],
                lhsT=w2_tile[:, 0:P].bitcast(FP8X4),
                lhsT_scale=w2_plane[:].bitcast(U8)[:, 0:P],
                rhs=words[:].bitcast(FP8X4),
                rhs_scale=plane[:],
                start=True,
                stop=True,
            )

        both = keep.tile([P, 2, T], F32, name="both")
        nc.scalar.copy(both[:, 0, :], windows[0][:, 0:T])
        for a, b in TOKEN_CHUNKS:
            bring = nc.vector.tensor_copy if a < T // 2 else nc.scalar.copy
            bring(both[:, 1, a:b], windows[1][:, a:b])
        c_in = {}
        for a, b in TOKEN_CHUNKS:
            c_in[a] = keep.tile([P, b - a, 2], F32, name="c_in_%d" % a, align_bytes=64)
            interleave = nc.vector.tensor_copy if a < T // 2 else nc.scalar.copy
            interleave(c_in[a][:], both[:, :, a:b].rearrange("p u n -> p n u"))

        bank_tags = [("last_sums_%d" % c0, 1) for c0, c1 in LAST_PIECES]
        bank_tags = bank_tags + [("spare", 1)] + [("sums", 2)] * 2 + [("turned", 2)] * 2
        banks = {}
        for a, b in TOKEN_CHUNKS:
            c_words = keep.tile([P, b - a], U32, name="c_words_%d" % a, align_bytes=64)
            c_plane = keep.tile([P, b - a], U8, name="c_plane_%d" % a, align_bytes=64)
            nc.vector.quantize_mx(
                out=c_words[:].bitcast(FP8X4),
                scales=c_plane[:],
                in_=c_in[a][:].rearrange("p n u -> p (n u)").bitcast(BF16),
            )
            for h in range(2):
                tag, bufs = bank_tags[len(banks)]
                banks[(a, h)] = psum.tile([P, b - a], F32, name=tag, bufs=bufs)
                nc.tensor.matmul_mx(
                    out=banks[(a, h)][:],
                    lhsT=w2_tile[:, P * h : P * (h + 1)].bitcast(FP8X4),
                    lhsT_scale=w2_plane[:].bitcast(U8)[:, P * h : P * (h + 1)],
                    rhs=c_words[:].bitcast(FP8X4),
                    rhs_scale=c_plane[:],
                    start=True,
                    stop=True,
                )
        for first, last in STORE_RANGES:
            for h in range(2):
                result = keep.tile([P, last - first], F32, name="result_%d_%d" % (first, h), align_bytes=DMA_ALIGN)
                empty = nc.vector.tensor_copy if first > 0 and h == 1 else nc.scalar.copy
                for a, b in TOKEN_CHUNKS:
                    if first <= a < last:
                        empty(result[:, a - first : b - first], banks[(a, h)][:])
                nc.sync.dma_start(out[P * h : P * (h + 1), first:last], result[:])
